import numpy as np, ml_dtypes
CORES = [36,164,52,180,100,228,116,244]
N = 8
BF = ml_dtypes.bfloat16
def gentries(a):
    return np.ascontiguousarray(a.reshape(8, 16, -1).transpose(0, 2, 1)).reshape(8, -1)
def gtable(e):
    e = np.asarray(e); return np.ascontiguousarray(e.reshape(8, -1, 16).transpose(0, 2, 1)).reshape(128, -1).astype(np.int32)
V, CAP, RO, DEC = 128, 32, 5, 8
S = N * V; E = 16 * S; D = 16 * N
def level(rng, *shape):
    return (256 * rng.random(shape[:2] + (1,) + shape[3:]) * rng.random(shape)).astype(np.int64)
def parts(rng):
    fan = np.argsort(rng.random((N, 8, E)), axis=-1)
    lo = rng.choice(np.array([0, 32, 96]), (N, 8, 1)); cost = lo + ((256 - lo) * rng.random((N, 8, E))).astype(np.int64)
    th = np.stack([rng.permutation(np.array([120, 250, 500, 900, 1300, 1600, 1800, 2000])) for q in range(N)]) + rng.integers(0, 40, (N, 8))
    x = level(rng, N, 8, 16, V); dv = np.where(rng.random((N, 8, 1, RO, V)) < 0.15, level(rng, N, 8, 16, RO, V), 0)
    return x, fan, cost, th, dv
def pack(x, fan, cost, th, dv):
    return {"x0": np.ascontiguousarray(x.reshape(N, 128, V)).astype(np.int32), "fan": np.stack([gtable(a) for a in fan]), "cost": np.ascontiguousarray(cost).astype(np.int32),
            "th": np.ascontiguousarray(np.repeat(th, 16, axis=1)[:, :, None]).astype(np.int32), "drv": np.ascontiguousarray(dv.reshape(N, 128, RO * V)).astype(np.int32)}
def setup_inputs(rng):
    return pack(*parts(rng))
def setup_inputs_room(rng):
    x, fan, cost, th, dv = parts(rng); th = rng.integers(200, 1501, (N, 8)); dv[:, :, :, 0] = 0
    for q in range(N):
        for g in range(8):
            o = rng.permutation(V); t = int(th[q, g]); n = int(rng.choice(np.array([0, 1, CAP - 1, CAP, CAP + 1, V])))
            if q == 0: n = (CAP, CAP + 1, V, CAP - 1, 1, 0, CAP, CAP + 1)[g]
            x[q, g][:, o[:n]] = DEC + (t + 15) // 16 + rng.integers(0, 100, (16, n))
            x[q, g][:, o[n:]] = rng.integers(0, DEC + (t - 1) // 16 + 1, (16, V - n))
    return pack(x, fan, cost, th, dv)
def setup_inputs_ties(rng):
    x, fan, cost, th, dv = parts(rng); th = rng.choice(np.array([1, 2, 15, 16, 17, 255, 1000, 3000]), (N, 8))
    share = np.where(np.arange(8) % 2 == 0, 0.7, 0.1)[None, :, None, None]
    goal = th[:, :, None, None] - 1 + np.where(rng.random((N, 8, 1, V)) < share, rng.integers(1, 3, (N, 8, 1, V)), 0)
    m = goal // 16; y = m + (np.arange(16)[:, None] < goal % 16)
    d = ((np.minimum(m, 254 - DEC - m) + 1) * rng.random((N, 8, 8, V))).astype(np.int64)
    y[:, :, :8] += d; y[:, :, 8:] -= d
    x = np.where(y > 0, y + DEC, rng.integers(0, DEC + 1, y.shape)); dv[:, :, :, 0] = 0
    th[:, 0] = 16 * DEC; th[:, 1] = 16 * DEC + 1
    x[:, :2] = rng.integers(RO * DEC + 1, 256, (N, 2, 16, V)); cost[:, :2] = 255; dv[:, :2] = 0
    x[:, 7] = 0; dv[:, 7] = 0; cost[:, 7] = rng.integers(254, 256, (N, E))
    for q in range(N):
        t = (4080, 4079, 4077, 2049)[q % 4]; th[q, 7] = t; o = rng.permutation(V)[:CAP]
        w = np.repeat(np.array([t - 1, t, 4080]), [CAP // 2, CAP // 4, CAP - CAP // 2 - CAP // 4])
        dv[q, 7][:, 0][:, o] = w // 16 + (np.arange(16)[:, None] < w % 16)
    return pack(x, fan, cost, th, dv)
def setup_inputs_alike(rng):
    x, fan, cost, th, dv = parts(rng); ar = np.arange(E); s = ar // 16; i = ar % 16
    fan[:, 0] = ar; fan[:, 1] = ar[::-1]; fan[:, 2] = (16 * (s // V) + i) * V + s % V
    for q in range(N): fan[q, 3] = (16 * rng.permutation(S)[:, None] + np.arange(16)).reshape(-1)
    fan[:, 5] = fan[0, 5].copy()
    cost[:, ::2] = rng.choice(np.array([0, 1, 254, 255]), (N, 4, E))
    c = cost[:, 2].reshape(N, D, V).copy(); h = c[:, :, ::2].shape[2]
    c[:, :D - 4, ::2] = rng.integers(254, 256, (N, D - 4, h)); c[:, D - 4:, ::2] = rng.integers(0, 2, (N, 4, h))
    cost[:, 2] = c.reshape(N, E); dv[:, 2, :, :, 0] = 0
    x = rng.choice(np.array([0, DEC - 1, DEC, DEC + 1, 128, 255]), (N, 8, 16, V)); x[..., 0] = 255; x[..., V - 1] = 255
    th = rng.choice(np.array([1, 16, 300, 600]), (N, 8)); th[:, 0] = 1; th[N - 1, 7] = 600
    return pack(x, fan, cost, th, dv)
def setup_inputs_quiet(rng):
    x, fan, cost, th, dv = parts(rng); x = np.minimum(x, 254); dv = np.minimum(dv, 254); h = rng.permutation(8); q = rng.permutation(N)
    th[q[0]] = 1; th[:, h[1]] = 1; th[q[1]] = 4080; th[q[1], h[2]] = 1; th[:, h[0]] = 4080
    x[:, h[1]] = 0; dv[:, h[1]] = 0; dv[q[0], h[1], :, 0, V - 1] = 254
    a = int(h[3]); x[:, a] = 0; dv[:, a, :, :2] = 0
    dv[:, a, :, 2] = np.where(rng.random((N, 1, V)) < 0.3, rng.integers(130, 255, (N, 16, V)), 0)
    b = int(h[4]); x[:, b] = 0; dv[:, b] = 0; cost[:, b] = rng.integers(200, 256, (N, E))
    th[:, b] = rng.integers(1000, 1601, N); th[q[1], b] = 4080; k = max(RO - 4, 0)
    for r in range(N):
        n = int(rng.integers(CAP // 2, CAP + 1)); o = rng.permutation(V)[:n]
        dv[r, b][:, k][:, o] = rng.integers(100, 121, (16, n)); dv[r, b][:, k + 1][:, o] = rng.integers(230, 255, (16, n))
    return pack(x, fan, cost, th, dv)
def setup_inputs_spread(rng):
    x, fan, cost, th, dv = parts(rng)
    x = np.minimum((np.exp2(8 * rng.random((N, 8, 1, V))) * rng.random((N, 8, 16, V))).astype(np.int64), 255)
    w = np.exp2(8 * rng.random((N, 8, E))); cost = np.minimum(np.where(rng.random((N, 8, E)) < 0.5, w - 1, 256 - w).astype(np.int64), 255)
    th = np.minimum(np.maximum(np.exp2(12 * rng.random((N, 8))).astype(np.int64), 1), 4080)
    v = np.minimum((np.exp2(8 * rng.random((N, 8, 1, RO, V))) * rng.random((N, 8, 16, RO, V))).astype(np.int64), 255)
    dv = np.where(rng.random((N, 8, 1, RO, V)) < 0.5 * rng.random((N, 8, 1, RO, 1)), v, 0)
    return pack(x, fan, cost, th, dv)
def check_inputs(d):
    bad = []
    for k, lo, hi in (("x0", 0, 255), ("fan", 0, E - 1), ("cost", 0, 255), ("th", 1, 4080), ("drv", 0, 255)):
        if np.min(d[k]) < lo or np.max(d[k]) > hi: bad.append("range of " + k)
    if not all(np.array_equal(np.sort(gentries(a), axis=1), np.tile(np.arange(E), (8, 1))) for a in d["fan"]): bad.append("every slot once in fan")
    t = d["th"].reshape(-1, 16)
    if np.any(t != t[:, :1]): bad.append("th alike in a group")
    return bad
def reference(x0, fan, cost, th, drv):
    x = x0.astype(np.int64).reshape(N, 8, 16, V); t = th.astype(np.int64).reshape(N, 8, 16)[:, :, :1]; dv = drv.astype(np.int64).reshape(N, 8, 16, RO, V)
    c = cost.astype(np.int16).reshape(N, 8, 1, D, V)
    fl = np.stack([gentries(a) for a in fan]).astype(np.int64).reshape(N, 8, S, 16)
    slots = np.zeros((N, 8, 16, E), np.int16); last = np.zeros((N, 8, 16, V), np.int64)
    for k in range(RO):
        best = np.stack([np.max(slots[r].reshape(8, 16, D, V) - c[r], axis=2) for r in range(N)]).astype(np.int64)
        x = np.maximum(np.maximum(x - DEC, dv[:, :, :, k]), np.maximum(best, 0))
        changed = np.add.reduce(np.abs(x - last), axis=2) >= t
        h = changed.astype(np.int64); sent = changed & (np.add.accumulate(h, axis=2) - h < CAP)
        last = np.where(sent[:, :, None, :], x, last)
        for g in range(8):
            s = np.flatnonzero(sent[:, g].reshape(-1))
            col = x[:, g].transpose(1, 0, 2).reshape(16, S)[:, s].astype(np.int16)
            for r in range(N):
                slots[r, g][:, fl[r, g][s]] = col[:, :, None]
    return {"yx": x.reshape(N, 128, V).astype(np.float32), "yl": last.reshape(N, 128, V).astype(np.float32)}

@@ -1,0 +1,344 @@
+from concourse.mybir import AluOpType, ActivationFunctionType
+
+N, V, CAP, RO, DEC = 8, 128, 32, 5, 8
+W = 131
+NP = V * W
+SPARE = 20992
+SL = 25216
+VV = V + CAP
+MS = 48
+MW = 34
+CH = 8 * W
+HALF = NP // 2
+
+SCRATCH = {
+    "slots": ("sbuf", [128, SL], "bfloat16"),
+    "dd": ("sbuf", [128, NP], "bfloat16"),
+    "outb": ("sbuf", [128, NP], "bfloat16"),
+    "fani": ("sbuf", [128, 1024], "int32"),
+    "fa": ("sbuf", [128, 1024], "int32"),
+    "post": ("sbuf", [128, 8 * VV], "float32"),
+    "ci": ("sbuf", [128, 1024], "int32"),
+    "cb": ("sbuf", [128, 1024], "bfloat16"),
+    "dq": ("sbuf", [128, CH], "bfloat16"),
+    "ddr": ("dram", [8, NP], "bfloat16"),
+    "x0i": ("sbuf", [128, 128], "int32"),
+    "drvi": ("sbuf", [128, 640], "int32"),
+    "thi": ("sbuf", [128, 4], "int32"),
+    "thf": ("sbuf", [128, 4], "float32"),
+    "xm": ("sbuf", [128, 128], "bfloat16"),
+    "xc": ("sbuf", [128, VV], "bfloat16"),
+    "ch": ("sbuf", [128, VV], "bfloat16"),
+    "cum": ("sbuf", [128, VV], "bfloat16"),
+    "junk": ("sbuf", [128, 2 * VV], "bfloat16"),
+    "acc": ("sbuf", [128, 8], "float32"),
+    "idxu": ("sbuf", [128, 8], "uint16"),
+    "colu": ("sbuf", [128, 16], "uint16"),
+    "offu": ("sbuf", [128, 258], "uint16"),
+    "vexp": ("sbuf", [128, 4128], "bfloat16"),
+    "msg": ("sbuf", [128, 4 * MS], "bfloat16"),
+    "land": ("sbuf", [128, 4 * 8 * MS], "bfloat16"),
+    "bm": ("sbuf", [128, 128], "bfloat16"),
+    "bh": ("sbuf", [128, 128], "bfloat16"),
+    "mg": ("sbuf", [128, 128], "bfloat16"),
+    "dm1": ("sbuf", [128, 136], "bfloat16"),
+    "dm": ("sbuf", [128, 136], "bfloat16"),
+    "sel": ("sbuf", [128, 1024], "bfloat16"),
+    "pc": ("sbuf", [128, 4], "int32"),
+    "colf": ("sbuf", [128, 4], "float32"),
+    "exi": ("sbuf", [128, 32], "int32"),
+    "exu": ("sbuf", [128, 34], "uint16"),
+    "yxf": ("sbuf", [128, 128], "float32"),
+    "ylf": ("sbuf", [128, 128], "float32"),
+    "dif": ("sbuf", [128, 128], "bfloat16"),
+    "chd": ("sbuf", [128, 128], "bfloat16"),
+    "uu": ("sbuf", [128, 128], "bfloat16"),
+    "tt": ("sbuf", [128, 128], "bfloat16"),
+    "psa": ("psum", [128, 1536], "float32"),
+    "psb": ("psum", [128, 1536], "float32"),
+    "pss": ("psum", [128, 512], "float32"),
+}
+SEMAPHORES = (["sv", "ss", "st", "sg", "lx", "ld", "lt", "lc", "lf", "ld2", "lq", "lb", "ox", "ol", "sent0", "sent1"]
+              + ["a%d_%d" % (m, k) for m in range(4) for k in range(1, N)])
+
+
+def rank_program(g, core, T, topo):
+    rank = T.rank_of(core)
+    if rank is None:
+        return
+    A, F = AluOpType, ActivationFunctionType
+    ve, sc, te, sy = g.vector, g.scalar, g.tensor, g.sync
+    Q = {"v": ve, "s": sc, "t": te, "y": sy, "g": g}
+    count = {}
+    seen = {q: {} for q in Q}
+
+    def wait(q, *toks):
+        for name, val in toks:
+            if seen[q].get(name, 0) < val:
+                Q[q].wait_ge(T.sem[name], val)
+                seen[q][name] = val
+
+    def inc(name, ins, n=1):
+        ins.then_inc(T.sem[name], n)
+        count[name] = count.get(name, 0) + n
+        return (name, count[name])
+
+    def V_(ins):
+        return inc("sv", ins)
+
+    def S_(ins):
+        return inc("ss", ins)
+
+    def P_(ins):
+        return inc("st", ins)
+
+    def G_(ins):
+        return inc("sg", ins)
+
+    slots, D, outb = T.slots, T.dd, T.outb
+    xo_ap = slots[:, 128:NP:W]
+    dr_ap = slots[:, 129:NP:W]
+    la_ap = slots[:, 130:NP:W]
+    xn_ap = outb[:, 129:NP:W]
+    mx_ap = outb[:, 130:NP:W]
+
+    t_x0 = inc("lx", sy.dma_start(T.x0i[:], T.x0[:]), 16)
+    t_dr = inc("ld", sy.dma_start(T.drvi[:, 0:256], T.drv[:, 0:256]), 16)
+    t_th = inc("lt", sy.dma_start(T.thi[:, 0:1], T.th[:]), 16)
+    for n in range(8):
+        t_ci = inc("lc", sy.dma_start(T.ci[:, n * 128:(n + 1) * 128], T.cost[n]), 16)
+    t_fan = inc("lf", sy.dma_start(T.fani[:], T.fan[:]), 16)
+
+    z1 = V_(ve.memset(slots[:, 0:1024], 0.0))
+    g_pc = G_(g.iota(T.pc[:, 0:1], [[0, 1]], 0, 1))
+    g_mg = G_(g.iota(T.mg[:], [[1, 8], [0, 16]], 0, 0, allow_small_or_imprecise_dtypes=True))
+    g_ex = G_(g.iota(T.exi[:], [[1, 32]], 0, 0))
+    wait("g", z1)
+    g_d1 = G_(g.affine_select(T.dm1[:, 0:W], slots[:, 0:W], [[1, W]], A.not_equal, 1.0, 0, -1))
+    g_du = G_(g.iota(T.post[:, 1024:1280], [[2048, 256]], 128 * SPARE, 128, allow_small_or_imprecise_dtypes=True))
+    wait("g", g_d1)
+    g_dm = G_(g.affine_select(T.dm[:, 0:W], T.dm1[:, 0:W], [[1, W]], A.not_equal, -1.0, -1, -1))
+    g_sel = G_(g.affine_select(T.sel[:], slots[:, 0:1024], [[-1, 8], [-16, 8], [0, 16]], A.not_equal, 1.0, -8, 1))
+
+    wait("s", z1)
+    for n in range(1, 4):
+        s_z = S_(sc.activation(slots[:, n * 1024:(n + 1) * 1024], slots[:, 0:1024], F.Copy))
+    V_(ve.memset(T.xc[:, V:VV], 0.0))
+    V_(ve.memset(T.ch[:, V:VV], 1.0))
+    V_(ve.memset(slots[:, 7168:8704], 0.0))
+    wait("v", g_pc)
+    V_(ve.tensor_scalar(T.pc[:, 1:2], T.pc[:, 0:1], 4, None, A.arith_shift_right))
+    v1 = V_(ve.tensor_scalar(T.pc[:, 2:3], T.pc[:, 0:1], 15, None, A.bitwise_and))
+    wait("v", g_ex)
+    V_(ve.tensor_copy(T.exu[:, 2:34], T.exi[:]))
+    wait("v", v1)
+    v2 = V_(ve.tensor_copy(T.colf[:, 0:1], T.pc[:, 1:2]))
+    V_(ve.tensor_scalar(T.colf[:, 1:2], T.pc[:, 2:3], 0.5, None, A.add))
+    V_(ve.tensor_scalar(T.colf[:, 2:3], T.pc[:, 2:3], 16.5, None, A.add))
+    V_(ve.tensor_copy(T.exu[:, 0:1], T.pc[:, 2:3]))
+    v_ex = V_(ve.tensor_scalar(T.exu[:, 1:2], T.pc[:, 2:3], 16.0, None, A.add))
+    wait("v", v2)
+    v_bm = V_(ve.tensor_scalar(T.bm[:], T.mg[:], T.colf[:, 0:1], None, A.is_equal))
+    V_(ve.tensor_scalar(T.bh[:], T.mg[:], T.colf[:, 0:1], -0.5, A.is_equal, A.mult))
+    V_(ve.memset(slots[:, 8704:10240], 0.0))
+
+    dests = [T.cores[(rank + k) % N] for k in range(N)]
+    arrive = [0] + [len(topo.engines(T.cores[(rank - k) % N], core)) for k in range(1, N)]
+    st = {}
+
+    def select(m, psum_tok, thcol, fill1, fill2, after_idx):
+        fill1()
+        wait("v", psum_tok)
+        v_ch = V_(ve.tensor_scalar(T.ch[:, 0:V], T.pss[:, 0:V], T.thf[:, thcol:thcol + 1], None, A.is_ge))
+        wait("v", v_ch)
+        v_cum = V_(ve.tensor_tensor_scan(T.cum[:], T.ch[:], T.ch[:], 0.0, A.add, A.max))
+        fill2()
+        wait("s", v_cum)
+        for h in range(2):
+            s_acc = S_(sc.activation(T.junk[:, h * VV:(h + 1) * VV], T.cum[:], F.Sign, bias=T.colf[:, 1 + h:2 + h],
+                                     scale=-1.0, accum_out=T.acc[:, 2 * m + h:2 * m + h + 1]))
+        acc = T.acc[:, 2 * m:2 * m + 2]
+        wait("s", s_acc)
+        s_idx = S_(sc.activation(T.msg[:, m * MS + 32:m * MS + 34], acc, F.Copy, bias=float(VV // 2), scale=0.5))
+        wait("v", s_acc)
+        v_idx = V_(ve.tensor_scalar(T.idxu[:, 2 * m:2 * m + 2], acc, 0.5, float(VV // 2), A.mult, A.add))
+        v_col = V_(ve.tensor_scalar(T.colu[:, 0:2], acc, 4.0, float(4 * VV + rank), A.mult, A.add))
+        V_(ve.tensor_scalar(T.offu[:, 0:2], acc, W / 2.0, float(VV // 2 * W + W - 1), A.mult, A.add))
+        wait("v", v_idx)
+        v_val = V_(ve.tensor_copy(T.msg[:, m * MS:m * MS + 32], T.xc[:, 0:VV].indirect(T.idxu[:, 2 * m:2 * m + 2])))
+        wait("g", s_idx, v_val)
+        sent = "sent0" if m == 0 else "sent1"
+        for k in range(1, N):
+            d = dests[k]
+            rid, pid = topo.addr(d, core)
+            o = (m * 8 + k) * MS
+            g.remote_dma(T.land[:, o:o + MW], T.msg[:, m * MS:m * MS + MW], T.sem["a%d_%d" % (m, k)], T.sem[sent],
+                         pid, rid, topo.mask(core, d))
+            count[sent] = count.get(sent, 0) + len(topo.engines(core, d))
+        wait("s", v_val, v_ex)
+        own = T.msg[:, m * MS:m * MS + 32]
+        s_e0 = (S_(sc.activation(T.vexp[:, 0:288], own.indirect(T.exu[:, 0:18]), F.Copy)),
+                S_(sc.activation(T.vexp[:, 288:544], own.indirect(T.exu[:, 18:34]), F.Copy)))
+        after_idx()
+        return v_col, s_e0
+
+    def push(m, v_col, s_e0):
+        s_e = {0: s_e0[0], 1: s_e0[1]}
+        arr = [None] + [("a%d_%d" % (m, k), arrive[k]) for k in range(1, N)]
+        for k in range(1, N):
+            count[arr[k][0]] = arr[k][1]
+            wait("s", arr[k])
+            win = T.land[:, (m * 8 + k) * MS:(m * 8 + k) * MS + 32]
+            o = 32 + 512 * k
+            if k == 1:
+                s_e[2] = S_(sc.activation(T.vexp[:, o:o + 256], win.indirect(T.exu[:, 2:18]), F.Copy))
+                s_e[3] = S_(sc.activation(T.vexp[:, o + 256:o + 512], win.indirect(T.exu[:, 18:34]), F.Copy))
+            else:
+                s_e[2 * k + 1] = S_(sc.activation(T.vexp[:, o:o + 512], win.indirect(T.exu[:, 2:34]), F.Copy))
+        ta, tb, last = {0: v_col}, {}, [("sv", count["sv"])]
+
+        def a(k):
+            wait("v", arr[k])
+            o = (m * 8 + k) * MS + 32
+            ta[k] = V_(ve.tensor_scalar(T.colu[:, 2 * k:2 * k + 2], T.land[:, o:o + 2], 8.0, float((rank - k) % N),
+                                        A.mult, A.add))
+
+        def b(k0, k1):
+            wait("v", ta[k1 - 1])
+            t = V_(ve.tensor_scalar(T.offu[:, 2 + 32 * k0:2 + 32 * k1], T.post[:].indirect(T.colu[:, 2 * k0:2 * k1]),
+                                    1.0 / 128, None, A.mult))
+            for k in range(k0, k1):
+                tb[k] = t
+
+        def d(h0, h1):
+            wait("v", tb[(h1 - 1) // 2], s_e[h1 - 1], last[0])
+            c0, c1 = (2 + 16 * h0 if h0 else 0), 2 + 16 * h1
+            last[0] = V_(ve.tensor_copy(slots[:, 0:SL].indirect(T.offu[:, c0:c1]), T.vexp[:, 16 * c0:16 * c1]))
+
+        b(0, 1); d(0, 1); d(1, 2)
+        a(1); b(1, 2); d(2, 3); d(3, 4)
+        a(2); a(3); b(2, 4); d(4, 6)
+        a(4); a(5); d(6, 8)
+        b(4, 6); a(6); a(7); d(8, 10)
+        b(6, 8); d(10, 16)
+        return last[0]
+
+    wait("v", t_x0)
+    v_xm = V_(ve.tensor_scalar(T.xm[:], T.x0i[:], -float(DEC), None, A.add))
+    wait("v", t_th)
+    V_(ve.tensor_copy(T.thf[:, 0:1], T.thi[:, 0:1]))
+    V_(ve.tensor_scalar(T.thf[:, 1:2], T.thi[:, 0:1], 0.5, None, A.mult))
+    wait("v", t_dr, v_xm)
+    v_x = V_(ve.tensor_tensor(T.xc[:, 0:V], T.xm[:], T.drvi[:, 0:V], A.max))
+    wait("t", v_x)
+    p_s = P_(te.matmul(T.pss[:, 0:V], T.bm[:], T.xc[:, 0:V], True, True))
+
+    def f1():
+        V_(ve.memset(slots[:, 10240:10880], 0.0))
+
+    def f2():
+        V_(ve.memset(slots[:, 10880:11776], 0.0))
+
+    def setup():
+        wait("v", t_ci)
+        v_cb = V_(ve.tensor_copy(T.cb[:], T.ci[:]))
+        wait("t", v_cb, g_dm)
+        for vl in range(8):
+            o = (vl // 3) * 512 + (vl % 3) * W
+            p_q = P_(te.matmul(T.psa[:, o:o + W], T.cb[:, vl:1024:8], T.dm[:, 0:W], True, True))
+        wait("s", p_q)
+        for bk in range(3):
+            n = min(3 * W, CH - bk * 3 * W)
+            s_q = S_(sc.activation(T.dq[:, bk * 3 * W:bk * 3 * W + n], T.psa[:, bk * 512:bk * 512 + n], F.Copy))
+        wait("s", s_q)
+        s_q = S_(sc.activation(T.dq[:, 0:CH:W], T.dq[:, 0:CH:W], F.Copy, bias=-512.0))
+        st["dq"] = s_q
+        for n in range(4, 7):
+            st["sz"] = S_(sc.activation(slots[:, n * 1024:(n + 1) * 1024], slots[:, 0:1024], F.Copy))
+        wait("y", s_q)
+        t_q = inc("lq", sy.dma_start(T.ddr[:], T.dq[:]), 16)
+        wait("y", ("sent0", count["sent0"]))
+        st["dr2"] = inc("ld2", sy.dma_start(T.drvi[:, 256:640], T.drv[:, 256:640]), 16)
+        wait("y", t_q)
+        for t in range(16):
+            st["db"] = inc("lb", sy.dma_start(D[t:128:16, 0:HALF], T.ddr[:, 0:HALF]), 16)
+        wait("v", t_fan)
+        v_a = V_(ve.tensor_scalar(T.fa[:], T.fani[:], 127, None, A.bitwise_and))
+        V_(ve.memset(slots[:, 11776:12288], 0.0))
+        wait("v", v_a)
+        V_(ve.tensor_scalar(T.psb[:, 0:512], T.fa[:, 0:512], float(128 * W - 1), None, A.mult))
+        v_a2 = V_(ve.tensor_scalar(T.psb[:, 512:1024], T.fa[:, 512:1024], float(128 * W - 1), None, A.mult))
+        V_(ve.memset(slots[:, 12288:12800], 0.0))
+        wait("v", v_a2)
+        for q in range(N):
+            st["post"] = V_(ve.tensor_tensor(T.post[:, q:1024:8], T.fani[:, q * 128:(q + 1) * 128],
+                                             T.psb[:, q * 128:(q + 1) * 128], A.add))
+        v_z = V_(ve.memset(slots[:, 12800:NP], 0.0))
+        wait("v", v_z, st["sz"], g_sel)
+        V_(ve.tensor_scalar(xo_ap, T.xc[:, 0:V], -float(DEC), None, A.add))
+        V_(ve.tensor_copy(dr_ap, T.drvi[:, V:2 * V]))
+
+    toks = select(0, p_s, 0, f1, f2, setup)
+
+    for t in range(1, RO):
+        v_last = push(t - 1, *toks)
+        if t == 1:
+            s_d = []
+            wait("t", st["dq"], g_sel)
+            for c in range(8):
+                ps = T.psa if c % 2 == 0 else T.psb
+                if c == 1:
+                    wait("t", st["post"])
+                if c >= 2:
+                    wait("t", s_d[c - 2])
+                for lo, hi in ((0, 512), (512, 1024), (1024, CH)):
+                    p_d = P_(te.matmul(ps[:, lo:hi], T.sel[:, c * 128:(c + 1) * 128], T.dq[:, lo:hi], True, True))
+                wait("s", p_d)
+                s_d.append(S_(sc.activation(D[:, HALF + c * CH:HALF + (c + 1) * CH], ps[:, 0:CH], F.Copy)))
+            pieces = [(0, HALF, st["db"])] + [(HALF + 2 * c * CH, HALF + (2 * c + 2) * CH, s_d[2 * c + 1]) for c in range(4)]
+        else:
+            pieces = [(0, HALF, v_last), (HALF, NP, v_last)]
+        wait("t", v_last)
+        p_l = P_(te.matmul(T.pss[:, 0:V], T.bh[:], la_ap, True, False))
+        wait("v", v_last)
+        for lo, hi, tok in pieces:
+            wait("v", tok)
+            v_scan = V_(ve.tensor_tensor_scan(outb[:, lo:hi], D[:, lo:hi], slots[:, lo:hi], 0.0, A.add, A.max))
+        wait("t", v_scan)
+        P_(te.matmul(T.pss[:, 0:V], T.bh[:], xn_ap, False, False))
+        p_s = P_(te.matmul(T.pss[:, 0:V], T.bm[:], mx_ap, False, True))
+        if t < RO - 1:
+            def g1():
+                wait("v", v_scan, p_l)
+                V_(ve.tensor_copy(T.xc[:, 0:V], xn_ap))
+                V_(ve.tensor_scalar(xo_ap, xn_ap, -float(DEC), None, A.add))
+
+            def g2():
+                wait("v", st["dr2"])
+                V_(ve.tensor_copy(dr_ap, T.drvi[:, (t + 1) * V:(t + 2) * V]))
+
+            toks = select(t, p_s, 1, g1, g2, lambda: None)
+        else:
+            wait("s", v_scan)
+            s_x = S_(sc.activation(T.yxf[:], xn_ap, F.Copy))
+            wait("s", s_x)
+            inc("ox", sc.dma_start(T.yx[:], T.yxf[:]), 16)
+            wait("v", v_scan)
+            V_(ve.tensor_tensor(T.dif[:], xn_ap, la_ap, A.subtract))
+            wait("v", p_s)
+            v_ch = V_(ve.tensor_scalar(T.ch[:, 0:V], T.pss[:, 0:V], T.thf[:, 1:2], None, A.is_ge))
+            wait("v", v_ch)
+            v_cum = V_(ve.tensor_tensor_scan(T.cum[:, 0:V], T.ch[:, 0:V], T.ch[:, 0:V], 0.0, A.add, A.max))
+            V_(ve.tensor_tensor(T.chd[:], T.ch[:, 0:V], T.dif[:], A.mult))
+            wait("v", v_cum)
+            v_u = V_(ve.tensor_scalar(T.uu[:], T.cum[:, 0:V], float(CAP), None, A.is_le))
+            wait("v", v_u)
+            v_t = V_(ve.tensor_tensor(T.tt[:], T.uu[:], T.chd[:], A.mult))
+            wait("v", v_t)
+            v_l = V_(ve.tensor_tensor(T.ylf[:], T.tt[:], la_ap, A.add))
+            wait("y", v_l)
+            inc("ol", sy.dma_start(T.yl[:], T.ylf[:]), 16)
+
+    for name in SEMAPHORES:
+        if name in count and name[0] != "a":
+            wait("g", (name, count[name]))

@@ -1,3 +1,4 @@
+from concourse.bass import DstId, RemoteDMATransfer
 from concourse.mybir import AluOpType, ActivationFunctionType
 
 N, V, CAP, RO, DEC = 8, 128, 32, 5, 8
@@ -9,14 +10,22 @@ VV = V + CAP
 MS = 48
 MW = 34
 CH = 8 * W
-HALF = NP // 2
+ND, DE = 8, 0
+C0, C1 = 8, 16
+ZD, ZG0 = 5120, 768
+ZV0, ZV1 = 2304, 1920
+POFF = 129 * (128 * W - 1)
+ZS0 = 384
 
 SCRATCH = {
     "slots": ("sbuf", [128, SL], "bfloat16"),
     "dd": ("sbuf", [128, NP], "bfloat16"),
     "outb": ("sbuf", [128, NP], "bfloat16"),
     "fani": ("sbuf", [128, 1024], "int32"),
-    "fa": ("sbuf", [128, 1024], "int32"),
+    "fa": ("sbuf", [128, 1024], "float32"),
+    "fh": ("sbuf", [128, 1024], "bfloat16"),
+    "zb": ("sbuf", [128, 128 * (16 - ND)], "bfloat16"),
+    "nid": ("sbuf", [128, 128], "bfloat16"),
     "post": ("sbuf", [128, 8 * VV], "float32"),
     "ci": ("sbuf", [128, 1024], "int32"),
     "cb": ("sbuf", [128, 1024], "bfloat16"),
@@ -35,7 +44,7 @@ SCRATCH = {
     "idxu": ("sbuf", [128, 8], "uint16"),
     "colu": ("sbuf", [128, 16], "uint16"),
     "offu": ("sbuf", [128, 258], "uint16"),
-    "vexp": ("sbuf", [128, 4128], "bfloat16"),
+    "vexp": ("sbuf", [128, 4096], "bfloat16"),
     "msg": ("sbuf", [128, 4 * MS], "bfloat16"),
     "land": ("sbuf", [128, 4 * 8 * MS], "bfloat16"),
     "bm": ("sbuf", [128, 128], "bfloat16"),
@@ -43,23 +52,33 @@ SCRATCH = {
     "mg": ("sbuf", [128, 128], "bfloat16"),
     "dm1": ("sbuf", [128, 136], "bfloat16"),
     "dm": ("sbuf", [128, 136], "bfloat16"),
-    "sel": ("sbuf", [128, 1024], "bfloat16"),
+    "sel": ("sbuf", [128, 128 * (16 - ND)], "bfloat16"),
     "pc": ("sbuf", [128, 4], "int32"),
     "colf": ("sbuf", [128, 4], "float32"),
     "exi": ("sbuf", [128, 32], "int32"),
-    "exu": ("sbuf", [128, 34], "uint16"),
+    "exu": ("sbuf", [128, 32], "uint16"),
     "yxf": ("sbuf", [128, 128], "float32"),
     "ylf": ("sbuf", [128, 128], "float32"),
     "dif": ("sbuf", [128, 128], "bfloat16"),
-    "chd": ("sbuf", [128, 128], "bfloat16"),
     "uu": ("sbuf", [128, 128], "bfloat16"),
-    "tt": ("sbuf", [128, 128], "bfloat16"),
     "psa": ("psum", [128, 1536], "float32"),
     "psb": ("psum", [128, 1536], "float32"),
     "pss": ("psum", [128, 512], "float32"),
 }
-SEMAPHORES = (["sv", "ss", "st", "sg", "lx", "ld", "lt", "lc", "lf", "ld2", "lq", "lb", "ox", "ol", "sent0", "sent1"]
-              + ["a%d_%d" % (m, k) for m in range(4) for k in range(1, N)])
+SEMAPHORES = (["sv", "ss", "st", "sg", "lx", "ld", "lt", "lc", "lf", "ld1", "ld2", "lq", "lb0", "lb1", "lz", "ox", "ol",
+               "sent0", "sent1", "lf1"] + ["a%d_%d" % (m, k) for m in range(4) for k in range(N)])
+
+
+def dst_id(dst, src, topo):
+    rid, pid = topo.addr(dst, src)
+    return DstId(rid=rid, pnc=pid)
+
+
+def to_ranks(T, topo, core, rank, m, ks):
+    dsts = [T.cores[(rank + k) % N] for k in ks]
+    return RemoteDMATransfer(dst_ids=[dst_id(d, core, topo) for d in dsts], dma_engine_mask=topo.mask(core, dsts[0]),
+                             remote_sem=T.sem["a%d_%d" % (m, rank)], srcs=[T.msg[:, m * MS:m * MS + MW]],
+                             dsts=[T.land[:, (m * 8 + k) * MS:(m * 8 + k) * MS + MW] for k in ks])
 
 
 def rank_program(g, core, T, topo):
@@ -103,44 +122,74 @@ def rank_program(g, core, T, topo):
     mx_ap = outb[:, 130:NP:W]
 
     t_x0 = inc("lx", sy.dma_start(T.x0i[:], T.x0[:]), 16)
-    t_dr = inc("ld", sy.dma_start(T.drvi[:, 0:256], T.drv[:, 0:256]), 16)
-    t_th = inc("lt", sy.dma_start(T.thi[:, 0:1], T.th[:]), 16)
+    t_dr = inc("ld", sc.dma_start(T.drvi[:, 0:V], T.drv[:, 0:V]), 16)
+    t_th = inc("lt", sc.dma_start(T.thi[:, 0:1], T.th[:]), 16)
+    t_fan = [inc(n, sy.dma_start(T.fani[:, h * 512:(h + 1) * 512], T.fan[:, h * 512:(h + 1) * 512]), 16)
+             for h, n in enumerate(("lf", "lf1"))]
     for n in range(8):
         t_ci = inc("lc", sy.dma_start(T.ci[:, n * 128:(n + 1) * 128], T.cost[n]), 16)
-    t_fan = inc("lf", sy.dma_start(T.fani[:], T.fan[:]), 16)
+    t_dr1 = inc("ld1", sy.dma_start(T.drvi[:, V:2 * V], T.drv[:, V:2 * V]), 16)
+
+    zc = [2048]
+
+    def take(n):
+        lo = zc[0]
+        zc[0] = min(NP, lo + n)
+        return lo, zc[0]
+
+    def zv(n):
+        lo, hi = take(n)
+        return V_(ve.memset(slots[:, lo:hi], 0.0))
+
+    def zs(n):
+        for k in range(0, n, 1024):
+            lo, hi = take(min(1024, n - k))
+            t = S_(sc.activation(slots[:, lo:hi], slots[:, 0:hi - lo], F.Copy))
+        return t
+
+    def zg(n):
+        lo, hi = take(n)
+        return G_(g.iota(slots[:, lo:hi], [[0, hi - lo]], 0, 0, allow_small_or_imprecise_dtypes=True))
 
     z1 = V_(ve.memset(slots[:, 0:1024], 0.0))
+    wait("v", ("sg", 1))
+    v1 = V_(ve.tensor_scalar(T.pc[:, 2:3], T.pc[:, 0:1], 15, None, A.bitwise_and))
+    t_zd = z2 = V_(ve.memset(slots[:, 1024:2048], 0.0))
+    for n in range(0, ZD, 2048):
+        wait("y", z2)
+        lo, hi = take(min(2048, ZD - n))
+        t_zd = inc("lz", sy.dma_start(slots[:, lo:hi], slots[:, 0:hi - lo]), 16)
+
     g_pc = G_(g.iota(T.pc[:, 0:1], [[0, 1]], 0, 1))
-    g_mg = G_(g.iota(T.mg[:], [[1, 8], [0, 16]], 0, 0, allow_small_or_imprecise_dtypes=True))
     g_ex = G_(g.iota(T.exi[:], [[1, 32]], 0, 0))
+    g_du = G_(g.iota(T.post[:, 1024:1280], [[16, 256]], SPARE - POFF, 1, allow_small_or_imprecise_dtypes=True))
     wait("g", z1)
+    g_b1 = G_(g.affine_select(T.mg[:], slots[:, 0:128], [[16, 8], [0, 16]], A.is_gt, 1.0, 0, -1))
     g_d1 = G_(g.affine_select(T.dm1[:, 0:W], slots[:, 0:W], [[1, W]], A.not_equal, 1.0, 0, -1))
-    g_du = G_(g.iota(T.post[:, 1024:1280], [[2048, 256]], 128 * SPARE, 128, allow_small_or_imprecise_dtypes=True))
+    wait("g", g_b1)
+    g_bm = G_(g.affine_select(T.bm[:], T.mg[:], [[16, 8], [0, 16]], A.is_ge, 0.0, 15, -1))
     wait("g", g_d1)
     g_dm = G_(g.affine_select(T.dm[:, 0:W], T.dm1[:, 0:W], [[1, W]], A.not_equal, -1.0, -1, -1))
-    g_sel = G_(g.affine_select(T.sel[:], slots[:, 0:1024], [[-1, 8], [-16, 8], [0, 16]], A.not_equal, 1.0, -8, 1))
+    g_z0 = zg(ZG0)
 
+    wait("v", v1, g_ex)
+    v2 = V_(ve.tensor_scalar(T.colf[:, 1:2], T.pc[:, 2:3], 0.5, None, A.add))
+    v_ex = V_(ve.tensor_copy(T.exu[:, 0:32], T.exi[:]))
+    zv(ZV0)
     wait("s", z1)
-    for n in range(1, 4):
-        s_z = S_(sc.activation(slots[:, n * 1024:(n + 1) * 1024], slots[:, 0:1024], F.Copy))
-    V_(ve.memset(T.xc[:, V:VV], 0.0))
-    V_(ve.memset(T.ch[:, V:VV], 1.0))
-    V_(ve.memset(slots[:, 7168:8704], 0.0))
-    wait("v", g_pc)
-    V_(ve.tensor_scalar(T.pc[:, 1:2], T.pc[:, 0:1], 4, None, A.arith_shift_right))
-    v1 = V_(ve.tensor_scalar(T.pc[:, 2:3], T.pc[:, 0:1], 15, None, A.bitwise_and))
-    wait("v", g_ex)
-    V_(ve.tensor_copy(T.exu[:, 2:34], T.exi[:]))
-    wait("v", v1)
-    v2 = V_(ve.tensor_copy(T.colf[:, 0:1], T.pc[:, 1:2]))
-    V_(ve.tensor_scalar(T.colf[:, 1:2], T.pc[:, 2:3], 0.5, None, A.add))
-    V_(ve.tensor_scalar(T.colf[:, 2:3], T.pc[:, 2:3], 16.5, None, A.add))
-    V_(ve.tensor_copy(T.exu[:, 0:1], T.pc[:, 2:3]))
-    v_ex = V_(ve.tensor_scalar(T.exu[:, 1:2], T.pc[:, 2:3], 16.0, None, A.add))
-    wait("v", v2)
-    v_bm = V_(ve.tensor_scalar(T.bm[:], T.mg[:], T.colf[:, 0:1], None, A.is_equal))
-    V_(ve.tensor_scalar(T.bh[:], T.mg[:], T.colf[:, 0:1], -0.5, A.is_equal, A.mult))
-    V_(ve.memset(slots[:, 8704:10240], 0.0))
+    S_(sc.activation(T.xc[:, V:VV], slots[:, 0:CAP], F.Copy))
+    s_ch = S_(sc.activation(T.ch[:, V:VV], slots[:, 0:CAP], F.Copy, bias=1.0))
+    for bk in range(3):
+        s_d0 = S_(sc.activation(T.psa[:, bk * 512:bk * 512 + 3 * W:W], slots[:, 0:3], F.Copy, bias=-512.0))
+    zs(1024)
+    wait("s", v2)
+    s_c2 = S_(sc.activation(T.colf[:, 2:3], T.colf[:, 1:2], F.Copy, bias=16.0))
+    zs(1024)
+    wait("s", g_bm)
+    s_bh = S_(sc.activation(T.bh[:], T.bm[:], F.Copy, scale=-0.5))
+    wait("s", g_d1)
+    s_ni = S_(sc.activation(T.nid[:], T.dm1[:, 0:128], F.Copy, scale=-float(128 * W)))
+    s_z = zs(ZS0)
 
     dests = [T.cores[(rank + k) % N] for k in range(N)]
     arrive = [0] + [len(topo.engines(T.cores[(rank - k) % N], core)) for k in range(1, N)]
@@ -150,10 +199,10 @@ def rank_program(g, core, T, topo):
         fill1()
         wait("v", psum_tok)
         v_ch = V_(ve.tensor_scalar(T.ch[:, 0:V], T.pss[:, 0:V], T.thf[:, thcol:thcol + 1], None, A.is_ge))
-        wait("v", v_ch)
+        wait("v", v_ch, s_ch)
         v_cum = V_(ve.tensor_tensor_scan(T.cum[:], T.ch[:], T.ch[:], 0.0, A.add, A.max))
         fill2()
-        wait("s", v_cum)
+        wait("s", v_cum, s_c2)
         for h in range(2):
             s_acc = S_(sc.activation(T.junk[:, h * VV:(h + 1) * VV], T.cum[:], F.Sign, bias=T.colf[:, 1 + h:2 + h],
                                      scale=-1.0, accum_out=T.acc[:, 2 * m + h:2 * m + h + 1]))
@@ -168,33 +217,25 @@ def rank_program(g, core, T, topo):
         v_val = V_(ve.tensor_copy(T.msg[:, m * MS:m * MS + 32], T.xc[:, 0:VV].indirect(T.idxu[:, 2 * m:2 * m + 2])))
         wait("g", s_idx, v_val)
         sent = "sent0" if m == 0 else "sent1"
-        for k in range(1, N):
-            d = dests[k]
-            rid, pid = topo.addr(d, core)
-            o = (m * 8 + k) * MS
-            g.remote_dma(T.land[:, o:o + MW], T.msg[:, m * MS:m * MS + MW], T.sem["a%d_%d" % (m, k)], T.sem[sent],
-                         pid, rid, topo.mask(core, d))
-            count[sent] = count.get(sent, 0) + len(topo.engines(core, d))
+        g.remote_dma_fused([to_ranks(T, topo, core, rank, m, range(1, N))], local_sem=T.sem[sent])
+        count[sent] = count.get(sent, 0) + len(topo.engines(core, dests[1]))
+        after_idx()
         wait("s", v_val, v_ex)
         own = T.msg[:, m * MS:m * MS + 32]
-        s_e0 = (S_(sc.activation(T.vexp[:, 0:288], own.indirect(T.exu[:, 0:18]), F.Copy)),
-                S_(sc.activation(T.vexp[:, 288:544], own.indirect(T.exu[:, 18:34]), F.Copy)))
-        after_idx()
+        s_e0 = (S_(sc.activation(T.vexp[:, 0:16 * C0], own.indirect(T.exu[:, 0:C0]), F.Copy)),
+                S_(sc.activation(T.vexp[:, 16 * C0:512], own.indirect(T.exu[:, C0:32]), F.Copy)))
         return v_col, s_e0
 
     def push(m, v_col, s_e0):
-        s_e = {0: s_e0[0], 1: s_e0[1]}
-        arr = [None] + [("a%d_%d" % (m, k), arrive[k]) for k in range(1, N)]
+        s_e = {C0: s_e0[0], 32: s_e0[1]}
+        arr = [None] + [("a%d_%d" % (m, (rank - k) % N), arrive[k]) for k in range(1, N)]
         for k in range(1, N):
             count[arr[k][0]] = arr[k][1]
             wait("s", arr[k])
             win = T.land[:, (m * 8 + k) * MS:(m * 8 + k) * MS + 32]
-            o = 32 + 512 * k
-            if k == 1:
-                s_e[2] = S_(sc.activation(T.vexp[:, o:o + 256], win.indirect(T.exu[:, 2:18]), F.Copy))
-                s_e[3] = S_(sc.activation(T.vexp[:, o + 256:o + 512], win.indirect(T.exu[:, 18:34]), F.Copy))
-            else:
-                s_e[2 * k + 1] = S_(sc.activation(T.vexp[:, o:o + 512], win.indirect(T.exu[:, 2:34]), F.Copy))
+            for c0, c1 in (((0, C1), (C1, 32)) if k == 1 else ((0, 32),)):
+                s_e[32 * k + c1] = S_(sc.activation(T.vexp[:, 512 * k + 16 * c0:512 * k + 16 * c1],
+                                                    win.indirect(T.exu[:, c0:c1]), F.Copy))
         ta, tb, last = {0: v_col}, {}, [("sv", count["sv"])]
 
         def a(k):
@@ -204,23 +245,24 @@ def rank_program(g, core, T, topo):
                                         A.mult, A.add))
 
         def b(k0, k1):
-            wait("v", ta[k1 - 1])
+            wait("v", ta[k1 - 1], st["post"])
             t = V_(ve.tensor_scalar(T.offu[:, 2 + 32 * k0:2 + 32 * k1], T.post[:].indirect(T.colu[:, 2 * k0:2 * k1]),
-                                    1.0 / 128, None, A.mult))
+                                    float(POFF), None, A.add))
             for k in range(k0, k1):
                 tb[k] = t
 
-        def d(h0, h1):
-            wait("v", tb[(h1 - 1) // 2], s_e[h1 - 1], last[0])
-            c0, c1 = (2 + 16 * h0 if h0 else 0), 2 + 16 * h1
-            last[0] = V_(ve.tensor_copy(slots[:, 0:SL].indirect(T.offu[:, c0:c1]), T.vexp[:, 16 * c0:16 * c1]))
+        def d(c0, c1):
+            wait("v", tb[(c1 - 1) // 32], s_e[c1], last[0])
+            last[0] = V_(ve.tensor_copy(slots[:, 0:SL].indirect(T.offu[:, 2 + c0:2 + c1]), T.vexp[:, 16 * c0:16 * c1]))
 
-        b(0, 1); d(0, 1); d(1, 2)
-        a(1); b(1, 2); d(2, 3); d(3, 4)
-        a(2); a(3); b(2, 4); d(4, 6)
-        a(4); a(5); d(6, 8)
-        b(4, 6); a(6); a(7); d(8, 10)
-        b(6, 8); d(10, 16)
+        b(0, 1)
+        wait("v", last[0])
+        last[0] = V_(ve.tensor_copy(slots[:, 0:SL].indirect(T.offu[:, 0:2]), T.msg[:, m * MS:m * MS + 32]))
+        d(0, C0); d(C0, 32)
+        a(1); b(1, 2); d(32, 32 + C1); a(2); a(3); d(32 + C1, 64)
+        b(2, 4); a(4); a(5); d(64, 128)
+        b(4, 6); a(6); a(7); d(128, 192)
+        b(6, 8); d(192, 256)
         return last[0]
 
     wait("v", t_x0)
@@ -230,75 +272,91 @@ def rank_program(g, core, T, topo):
     V_(ve.tensor_scalar(T.thf[:, 1:2], T.thi[:, 0:1], 0.5, None, A.mult))
     wait("v", t_dr, v_xm)
     v_x = V_(ve.tensor_tensor(T.xc[:, 0:V], T.xm[:], T.drvi[:, 0:V], A.max))
-    wait("t", v_x)
+    wait("t", v_x, g_bm)
     p_s = P_(te.matmul(T.pss[:, 0:V], T.bm[:], T.xc[:, 0:V], True, True))
+    s_d = []
 
-    def f1():
-        V_(ve.memset(slots[:, 10240:10880], 0.0))
+    def dchunk(c):
+        ps = T.psa if c % 2 == 0 else T.psb
+        wait("t", st["dq"], st["sel"])
+        if c == 1:
+            wait("t", st["post"])
+        if c >= 2:
+            wait("t", s_d[c - 2])
+        for lo, hi in ((0, 512), (512, 1024), (1024, CH)):
+            p_d = P_(te.matmul(ps[:, lo:hi], T.sel[:, c * 128:(c + 1) * 128], T.dq[:, lo:hi], True, True))
+        wait("s", p_d)
+        s_d.append(S_(sc.activation(D[:, (ND + c) * CH:(ND + c + 1) * CH], ps[:, 0:CH], F.Copy)))
 
-    def f2():
-        V_(ve.memset(slots[:, 10880:11776], 0.0))
+    def fan1(h):
+        wait("v", t_fan[h])
+        c = slice(h * 512, (h + 1) * 512)
+        st["fa%d" % h] = V_(ve.tensor_scalar(T.fa[:, c], T.fani[:, c], float(W), None, A.mult))
 
     def setup():
+        wait("g", G_(g.iota(T.zb[:], [[0, 128 * (16 - ND)]], 0, 0, allow_small_or_imprecise_dtypes=True)))
+        st["gz"] = g_z0
+        st["sel"] = G_(g.affine_select(T.sel[:], T.zb[:], [[-1, 16 - ND], [-16, 8], [0, 16]], A.not_equal, 1.0, -ND, 1))
+        p_f = []
+        fan1(1)
+        for h in range(2):
+            c = slice(h * 512, (h + 1) * 512)
+            wait("s", st["fa%d" % h])
+            s_h = S_(sc.activation(T.fh[:, c], T.fa[:, c], F.Copy, bias=128.504, scale=1.0 / (128 * W)))
+            wait("t", s_h, s_ni)
+            P_(te.matmul(T.psb[:, c], T.nid[:], T.fh[:, c], True, False))
+            p_f.append(P_(te.matmul(T.psb[:, c], T.dm1[:, 0:128], T.fh[:, c], False, True)))
+        st["pf"] = p_f
+
+    def setup2():
+        lo, hi = NP - ZV1, NP
+        v_z = V_(ve.memset(slots[:, lo:hi], 0.0))
         wait("v", t_ci)
         v_cb = V_(ve.tensor_copy(T.cb[:], T.ci[:]))
-        wait("t", v_cb, g_dm)
-        for vl in range(8):
-            o = (vl // 3) * 512 + (vl % 3) * W
-            p_q = P_(te.matmul(T.psa[:, o:o + W], T.cb[:, vl:1024:8], T.dm[:, 0:W], True, True))
-        wait("s", p_q)
+        for q in range(N):
+            wait("v", st["pf"][q // 4], g_du)
+            st["post"] = V_(ve.tensor_tensor(T.post[:, q:1024:8], T.fa[:, q * 128:(q + 1) * 128],
+                                             T.psb[:, q * 128:(q + 1) * 128], A.add))
+        wait("t", v_cb, g_dm, s_d0)
+        ZS1 = lo - zc[0]
+        st["sz"] = zs(ZS1) if ZS1 else s_z
         for bk in range(3):
+            for vl in range(3 * bk, min(8, 3 * bk + 3)):
+                o = bk * 512 + (vl % 3) * W
+                p_q = P_(te.matmul(T.psa[:, o + 1:o + W], T.cb[:, vl:1024:8], T.dm[:, 1:W], True, True))
+            wait("s", p_q)
             n = min(3 * W, CH - bk * 3 * W)
             s_q = S_(sc.activation(T.dq[:, bk * 3 * W:bk * 3 * W + n], T.psa[:, bk * 512:bk * 512 + n], F.Copy))
-        wait("s", s_q)
-        s_q = S_(sc.activation(T.dq[:, 0:CH:W], T.dq[:, 0:CH:W], F.Copy, bias=-512.0))
         st["dq"] = s_q
-        for n in range(4, 7):
-            st["sz"] = S_(sc.activation(slots[:, n * 1024:(n + 1) * 1024], slots[:, 0:1024], F.Copy))
         wait("y", s_q)
         t_q = inc("lq", sy.dma_start(T.ddr[:], T.dq[:]), 16)
-        wait("y", ("sent0", count["sent0"]))
-        st["dr2"] = inc("ld2", sy.dma_start(T.drvi[:, 256:640], T.drv[:, 256:640]), 16)
         wait("y", t_q)
-        for t in range(16):
-            st["db"] = inc("lb", sy.dma_start(D[t:128:16, 0:HALF], T.ddr[:, 0:HALF]), 16)
-        wait("v", t_fan)
-        v_a = V_(ve.tensor_scalar(T.fa[:], T.fani[:], 127, None, A.bitwise_and))
-        V_(ve.memset(slots[:, 11776:12288], 0.0))
-        wait("v", v_a)
-        V_(ve.tensor_scalar(T.psb[:, 0:512], T.fa[:, 0:512], float(128 * W - 1), None, A.mult))
-        v_a2 = V_(ve.tensor_scalar(T.psb[:, 512:1024], T.fa[:, 512:1024], float(128 * W - 1), None, A.mult))
-        V_(ve.memset(slots[:, 12288:12800], 0.0))
-        wait("v", v_a2)
-        for q in range(N):
-            st["post"] = V_(ve.tensor_tensor(T.post[:, q:1024:8], T.fani[:, q * 128:(q + 1) * 128],
-                                             T.psb[:, q * 128:(q + 1) * 128], A.add))
-        v_z = V_(ve.memset(slots[:, 12800:NP], 0.0))
-        wait("v", v_z, st["sz"], g_sel)
+        for w in range(2):
+            lo, hi = w * ND // 2 * CH, (w + 1) * ND // 2 * CH
+            for t in range(16):
+                st["db%d" % w] = inc("lb%d" % w, sy.dma_start(D[t:128:16, lo:hi], T.ddr[:, lo:hi]), 16)
+        st["dr2"] = inc("ld2", sy.dma_start(T.drvi[:, 2 * V:640], T.drv[:, 2 * V:640]), 16)
+        wait("v", v_z, st["sz"], st["gz"], t_zd, t_dr1)
         V_(ve.tensor_scalar(xo_ap, T.xc[:, 0:V], -float(DEC), None, A.add))
         V_(ve.tensor_copy(dr_ap, T.drvi[:, V:2 * V]))
 
-    toks = select(0, p_s, 0, f1, f2, setup)
+    toks = select(0, p_s, 0, lambda: zv(640), lambda: fan1(0), setup)
+    setup2()
 
     for t in range(1, RO):
+        if t == 1:
+            for c in range(DE):
+                dchunk(c)
         v_last = push(t - 1, *toks)
         if t == 1:
-            s_d = []
-            wait("t", st["dq"], g_sel)
-            for c in range(8):
-                ps = T.psa if c % 2 == 0 else T.psb
-                if c == 1:
-                    wait("t", st["post"])
-                if c >= 2:
-                    wait("t", s_d[c - 2])
-                for lo, hi in ((0, 512), (512, 1024), (1024, CH)):
-                    p_d = P_(te.matmul(ps[:, lo:hi], T.sel[:, c * 128:(c + 1) * 128], T.dq[:, lo:hi], True, True))
-                wait("s", p_d)
-                s_d.append(S_(sc.activation(D[:, HALF + c * CH:HALF + (c + 1) * CH], ps[:, 0:CH], F.Copy)))
-            pieces = [(0, HALF, st["db"])] + [(HALF + 2 * c * CH, HALF + (2 * c + 2) * CH, s_d[2 * c + 1]) for c in range(4)]
+            for c in range(DE, 16 - ND):
+                dchunk(c)
+            pieces = [(ND * CH, (ND + DE) * CH, s_d[DE - 1])] if DE else []
+            late = [((ND + c) * CH, (ND + c + 2) * CH, s_d[c + 1]) for c in range(DE, 16 - ND, 2)]
+            pieces += [(0, ND // 2 * CH, st["db0"]), late[0], (ND // 2 * CH, ND * CH, st["db1"])] + late[1:]
         else:
-            pieces = [(0, HALF, v_last), (HALF, NP, v_last)]
-        wait("t", v_last)
+            pieces = [(0, NP, v_last)]
+        wait("t", v_last, s_bh)
         p_l = P_(te.matmul(T.pss[:, 0:V], T.bh[:], la_ap, True, False))
         wait("v", v_last)
         for lo, hi, tok in pieces:
@@ -329,13 +387,13 @@ def rank_program(g, core, T, topo):
             v_ch = V_(ve.tensor_scalar(T.ch[:, 0:V], T.pss[:, 0:V], T.thf[:, 1:2], None, A.is_ge))
             wait("v", v_ch)
             v_cum = V_(ve.tensor_tensor_scan(T.cum[:, 0:V], T.ch[:, 0:V], T.ch[:, 0:V], 0.0, A.add, A.max))
-            V_(ve.tensor_tensor(T.chd[:], T.ch[:, 0:V], T.dif[:], A.mult))
+            V_(ve.tensor_tensor(T.psa[:, 0:V], T.ch[:, 0:V], T.dif[:], A.mult))
             wait("v", v_cum)
             v_u = V_(ve.tensor_scalar(T.uu[:], T.cum[:, 0:V], float(CAP), None, A.is_le))
             wait("v", v_u)
-            v_t = V_(ve.tensor_tensor(T.tt[:], T.uu[:], T.chd[:], A.mult))
+            v_t = V_(ve.tensor_tensor(T.psb[:, 0:V], T.uu[:], T.psa[:, 0:V], A.mult))
             wait("v", v_t)
-            v_l = V_(ve.tensor_tensor(T.ylf[:], T.tt[:], la_ap, A.add))
+            v_l = V_(ve.tensor_tensor(T.ylf[:], T.psb[:, 0:V], la_ap, A.add))
             wait("y", v_l)
             inc("ol", sy.dma_start(T.yl[:], T.ylf[:]), 16)
 

@@ -2,20 +2,21 @@ from concourse.bass import DstId, RemoteDMATransfer
 from concourse.mybir import AluOpType, ActivationFunctionType
 
 N, V, CAP, RO, DEC = 8, 128, 32, 5, 8
-W = 131
+W = 130
 NP = V * W
 SPARE = 20992
 SL = 25216
 VV = V + CAP
-MS = 48
-MW = 34
+MS = 80
+MW = 41
+VA = V - 16
 CH = 8 * W
-ND, DE = 8, 0
-C0, C1 = 8, 16
-ZD, ZG0 = 5120, 768
-ZV0, ZV1 = 2304, 1920
+ND = 8
+C0 = 8
+ZD, ZG0 = 8192, 384
+ZV0, ZV1 = 1792, 896
+ZS0 = 128
 POFF = 129 * (128 * W - 1)
-ZS0 = 384
 
 SCRATCH = {
     "slots": ("sbuf", [128, SL], "bfloat16"),
@@ -36,6 +37,7 @@ SCRATCH = {
     "thi": ("sbuf", [128, 4], "int32"),
     "thf": ("sbuf", [128, 4], "float32"),
     "xm": ("sbuf", [128, 128], "bfloat16"),
+    "xd": ("sbuf", [128, 128], "bfloat16"),
     "xc": ("sbuf", [128, VV], "bfloat16"),
     "ch": ("sbuf", [128, VV], "bfloat16"),
     "cum": ("sbuf", [128, VV], "bfloat16"),
@@ -64,21 +66,10 @@ SCRATCH = {
     "psa": ("psum", [128, 1536], "float32"),
     "psb": ("psum", [128, 1536], "float32"),
     "pss": ("psum", [128, 512], "float32"),
+    "pst": ("psum", [128, 512], "float32"),
 }
-SEMAPHORES = (["sv", "ss", "st", "sg", "lx", "ld", "lt", "lc", "lf", "ld1", "ld2", "lq", "lb0", "lb1", "lz", "ox", "ol",
-               "sent0", "sent1", "lf1"] + ["a%d_%d" % (m, k) for m in range(4) for k in range(N)])
-
-
-def dst_id(dst, src, topo):
-    rid, pid = topo.addr(dst, src)
-    return DstId(rid=rid, pnc=pid)
-
-
-def to_ranks(T, topo, core, rank, m, ks):
-    dsts = [T.cores[(rank + k) % N] for k in ks]
-    return RemoteDMATransfer(dst_ids=[dst_id(d, core, topo) for d in dsts], dma_engine_mask=topo.mask(core, dsts[0]),
-                             remote_sem=T.sem["a%d_%d" % (m, rank)], srcs=[T.msg[:, m * MS:m * MS + MW]],
-                             dsts=[T.land[:, (m * 8 + k) * MS:(m * 8 + k) * MS + MW] for k in ks])
+SEMAPHORES = (["sv", "ss", "st", "sg", "lx", "ld", "lt", "lc", "lf", "lf1", "ld2", "lq", "lb0", "lb1", "lz", "ox", "ol",
+               "sent0", "sent1"] + ["a%d_%d" % (m, k) for m in range(4) for k in range(N)])
 
 
 def rank_program(g, core, T, topo):
@@ -92,7 +83,10 @@ def rank_program(g, core, T, topo):
     seen = {q: {} for q in Q}
 
     def wait(q, *toks):
+        most = {}
         for name, val in toks:
+            most[name] = max(most.get(name, 0), val)
+        for name, val in most.items():
             if seen[q].get(name, 0) < val:
                 Q[q].wait_ge(T.sem[name], val)
                 seen[q][name] = val
@@ -116,19 +110,16 @@ def rank_program(g, core, T, topo):
 
     slots, D, outb = T.slots, T.dd, T.outb
     xo_ap = slots[:, 128:NP:W]
-    dr_ap = slots[:, 129:NP:W]
-    la_ap = slots[:, 130:NP:W]
-    xn_ap = outb[:, 129:NP:W]
-    mx_ap = outb[:, 130:NP:W]
+    la_ap = slots[:, 129:NP:W]
+    xn_ap = outb[:, 128:NP:W]
 
     t_x0 = inc("lx", sy.dma_start(T.x0i[:], T.x0[:]), 16)
-    t_dr = inc("ld", sc.dma_start(T.drvi[:, 0:V], T.drv[:, 0:V]), 16)
+    t_dr = inc("ld", sc.dma_start(T.drvi[:, 0:2 * V], T.drv[:, 0:2 * V]), 16)
     t_th = inc("lt", sc.dma_start(T.thi[:, 0:1], T.th[:]), 16)
     t_fan = [inc(n, sy.dma_start(T.fani[:, h * 512:(h + 1) * 512], T.fan[:, h * 512:(h + 1) * 512]), 16)
              for h, n in enumerate(("lf", "lf1"))]
     for n in range(8):
         t_ci = inc("lc", sy.dma_start(T.ci[:, n * 128:(n + 1) * 128], T.cost[n]), 16)
-    t_dr1 = inc("ld1", sy.dma_start(T.drvi[:, V:2 * V], T.drv[:, V:2 * V]), 16)
 
     zc = [2048]
 
@@ -147,10 +138,6 @@ def rank_program(g, core, T, topo):
             t = S_(sc.activation(slots[:, lo:hi], slots[:, 0:hi - lo], F.Copy))
         return t
 
-    def zg(n):
-        lo, hi = take(n)
-        return G_(g.iota(slots[:, lo:hi], [[0, hi - lo]], 0, 0, allow_small_or_imprecise_dtypes=True))
-
     z1 = V_(ve.memset(slots[:, 0:1024], 0.0))
     wait("v", ("sg", 1))
     v1 = V_(ve.tensor_scalar(T.pc[:, 2:3], T.pc[:, 0:1], 15, None, A.bitwise_and))
@@ -160,9 +147,11 @@ def rank_program(g, core, T, topo):
         lo, hi = take(min(2048, ZD - n))
         t_zd = inc("lz", sy.dma_start(slots[:, lo:hi], slots[:, 0:hi - lo]), 16)
 
-    g_pc = G_(g.iota(T.pc[:, 0:1], [[0, 1]], 0, 1))
-    g_ex = G_(g.iota(T.exi[:], [[1, 32]], 0, 0))
-    g_du = G_(g.iota(T.post[:, 1024:1280], [[16, 256]], SPARE - POFF, 1, allow_small_or_imprecise_dtypes=True))
+    G_(g.iota(T.pc[:, 0:1], [[0, 1]], 0, 1))
+    g_ex = G_(g.iota(T.exi[:], [[1, 32]], 1, 0))
+    for h in range(2):
+        g_du = G_(g.iota(T.post[:, 640 * h + 512:640 * h + 640], [[16, 128]], SPARE + 2048 * h - POFF, 1,
+                         allow_small_or_imprecise_dtypes=True))
     wait("g", z1)
     g_b1 = G_(g.affine_select(T.mg[:], slots[:, 0:128], [[16, 8], [0, 16]], A.is_gt, 1.0, 0, -1))
     g_d1 = G_(g.affine_select(T.dm1[:, 0:W], slots[:, 0:W], [[1, W]], A.not_equal, 1.0, 0, -1))
@@ -170,7 +159,8 @@ def rank_program(g, core, T, topo):
     g_bm = G_(g.affine_select(T.bm[:], T.mg[:], [[16, 8], [0, 16]], A.is_ge, 0.0, 15, -1))
     wait("g", g_d1)
     g_dm = G_(g.affine_select(T.dm[:, 0:W], T.dm1[:, 0:W], [[1, W]], A.not_equal, -1.0, -1, -1))
-    g_z0 = zg(ZG0)
+    lo, hi = take(ZG0)
+    g_z = G_(g.iota(slots[:, lo:hi], [[0, hi - lo]], 0, 0, allow_small_or_imprecise_dtypes=True))
 
     wait("v", v1, g_ex)
     v2 = V_(ve.tensor_scalar(T.colf[:, 1:2], T.pc[:, 2:3], 0.5, None, A.add))
@@ -178,71 +168,85 @@ def rank_program(g, core, T, topo):
     zv(ZV0)
     wait("s", z1)
     S_(sc.activation(T.xc[:, V:VV], slots[:, 0:CAP], F.Copy))
+    s_ms = S_(sc.activation(T.msg[:], slots[:, 0:4 * MS], F.Copy))
     s_ch = S_(sc.activation(T.ch[:, V:VV], slots[:, 0:CAP], F.Copy, bias=1.0))
     for bk in range(3):
         s_d0 = S_(sc.activation(T.psa[:, bk * 512:bk * 512 + 3 * W:W], slots[:, 0:3], F.Copy, bias=-512.0))
     zs(1024)
     wait("s", v2)
     s_c2 = S_(sc.activation(T.colf[:, 2:3], T.colf[:, 1:2], F.Copy, bias=16.0))
-    zs(1024)
+    zs(768)
     wait("s", g_bm)
     s_bh = S_(sc.activation(T.bh[:], T.bm[:], F.Copy, scale=-0.5))
     wait("s", g_d1)
     s_ni = S_(sc.activation(T.nid[:], T.dm1[:, 0:128], F.Copy, scale=-float(128 * W)))
-    s_z = zs(ZS0)
+    zs(ZS0)
 
-    dests = [T.cores[(rank + k) % N] for k in range(N)]
-    arrive = [0] + [len(topo.engines(T.cores[(rank - k) % N], core)) for k in range(1, N)]
+    peers = [T.cores[rank ^ k] for k in range(N)]
+    ids = [DstId(rid=topo.addr(d, core)[0], pnc=topo.addr(d, core)[1]) for d in peers[1:]]
+    odd = rank % 2
     st = {}
 
-    def select(m, psum_tok, thcol, fill1, fill2, after_idx):
-        fill1()
-        wait("v", psum_tok)
-        v_ch = V_(ve.tensor_scalar(T.ch[:, 0:V], T.pss[:, 0:V], T.thf[:, thcol:thcol + 1], None, A.is_ge))
-        wait("v", v_ch, s_ch)
-        v_cum = V_(ve.tensor_tensor_scan(T.cum[:], T.ch[:], T.ch[:], 0.0, A.add, A.max))
-        fill2()
+    def changed(lo, hi, ps, tok, thcol):
+        wait("v", tok)
+        return V_(ve.tensor_scalar(T.ch[:, lo:hi], ps[:, lo:hi], T.thf[:, thcol:thcol + 1], None, A.is_ge))
+
+    def counts(lo, hi, *toks):
+        wait("v", s_ch, *toks)
+        return V_(ve.tensor_tensor_scan(T.cum[:, lo:hi], T.ch[:, lo:hi], T.ch[:, lo:hi],
+                                        T.cum[:, lo - 1:lo] if lo else 0.0, A.add, A.max))
+
+    def select(m, v_cum, after_send):
         wait("s", v_cum, s_c2)
         for h in range(2):
             s_acc = S_(sc.activation(T.junk[:, h * VV:(h + 1) * VV], T.cum[:], F.Sign, bias=T.colf[:, 1 + h:2 + h],
                                      scale=-1.0, accum_out=T.acc[:, 2 * m + h:2 * m + h + 1]))
         acc = T.acc[:, 2 * m:2 * m + 2]
         wait("s", s_acc)
-        s_idx = S_(sc.activation(T.msg[:, m * MS + 32:m * MS + 34], acc, F.Copy, bias=float(VV // 2), scale=0.5))
+        s_idx = S_(sc.activation(T.msg[:, m * MS:m * MS + MW:MS // 2], acc, F.Copy, bias=float(VV // 2 - odd * VV), scale=0.5))
         wait("v", s_acc)
         v_idx = V_(ve.tensor_scalar(T.idxu[:, 2 * m:2 * m + 2], acc, 0.5, float(VV // 2), A.mult, A.add))
-        v_col = V_(ve.tensor_scalar(T.colu[:, 0:2], acc, 4.0, float(4 * VV + rank), A.mult, A.add))
+        v_col = V_(ve.tensor_scalar(T.colu[:, 0:2], acc, 2.0, float(2 * VV + 4 * VV * (1 - odd) + rank // 2), A.mult, A.add))
         V_(ve.tensor_scalar(T.offu[:, 0:2], acc, W / 2.0, float(VV // 2 * W + W - 1), A.mult, A.add))
         wait("v", v_idx)
-        v_val = V_(ve.tensor_copy(T.msg[:, m * MS:m * MS + 32], T.xc[:, 0:VV].indirect(T.idxu[:, 2 * m:2 * m + 2])))
+        v_val = V_(ve.tensor_copy(T.msg[:, m * MS + 1:m * MS + 33], T.xc[:, 0:VV].indirect(T.idxu[:, 2 * m:2 * m + 2])))
         wait("g", s_idx, v_val)
         sent = "sent0" if m == 0 else "sent1"
-        g.remote_dma_fused([to_ranks(T, topo, core, rank, m, range(1, N))], local_sem=T.sem[sent])
-        count[sent] = count.get(sent, 0) + len(topo.engines(core, dests[1]))
-        after_idx()
-        wait("s", v_val, v_ex)
-        own = T.msg[:, m * MS:m * MS + 32]
+        g.remote_dma_fused([RemoteDMATransfer(
+            dst_ids=ids, dma_engine_mask=topo.mask(core, peers[1]), remote_sem=T.sem["a%d_%d" % (m, rank)],
+            srcs=[T.msg[:, m * MS:m * MS + MW]],
+            dsts=[T.land[:, (m * 8 + k) * MS:(m * 8 + k) * MS + MW] for k in range(1, N)])], local_sem=T.sem[sent])
+        count[sent] = count.get(sent, 0) + len(topo.engines(core, peers[1]))
+        after_send()
+        wait("s", v_val, v_ex, s_idx)
+        own = T.msg[:, m * MS:m * MS + 33]
         s_e0 = (S_(sc.activation(T.vexp[:, 0:16 * C0], own.indirect(T.exu[:, 0:C0]), F.Copy)),
                 S_(sc.activation(T.vexp[:, 16 * C0:512], own.indirect(T.exu[:, C0:32]), F.Copy)))
         return v_col, s_e0
 
     def push(m, v_col, s_e0):
         s_e = {C0: s_e0[0], 32: s_e0[1]}
-        arr = [None] + [("a%d_%d" % (m, (rank - k) % N), arrive[k]) for k in range(1, N)]
-        for k in range(1, N):
-            count[arr[k][0]] = arr[k][1]
+        arr = [None] + [("a%d_%d" % (m, rank ^ k), len(topo.engines(peers[k], core))) for k in range(1, N)]
+        for k in range(1, 3):
             wait("s", arr[k])
-            win = T.land[:, (m * 8 + k) * MS:(m * 8 + k) * MS + 32]
-            for c0, c1 in (((0, C1), (C1, 32)) if k == 1 else ((0, 32),)):
-                s_e[32 * k + c1] = S_(sc.activation(T.vexp[:, 512 * k + 16 * c0:512 * k + 16 * c1],
-                                                    win.indirect(T.exu[:, c0:c1]), F.Copy))
+            win = T.land[:, (m * 8 + k) * MS:(m * 8 + k) * MS + 33]
+            s_e[32 * k + 32] = S_(sc.activation(T.vexp[:, 512 * k:512 * k + 512], win.indirect(T.exu[:, 0:32]), F.Copy))
+        wait("t", st["post"], st["dq"])
+        for k0, k1, ps, c in ((3, 4, T.psa, 0), (4, 6, T.psa, 512), (6, 8, T.psb, 0)):
+            for k in range(k0, k1):
+                wait("t", arr[k])
+                o, b0 = (m * 8 + k) * MS, c + 512 * (k - k0)
+                for i in range(16):
+                    p_e = P_(te.matmul(ps[:, b0 + i:b0 + 512:16], T.dm1[:, 0:128], T.land[:, o + 1:o + 33], True, True))
+            wait("s", p_e)
+            st["se"] = s_e[32 * k1] = S_(sc.activation(T.vexp[:, 512 * k0:512 * k1], ps[:, c:c + 512 * (k1 - k0)], F.Copy))
         ta, tb, last = {0: v_col}, {}, [("sv", count["sv"])]
 
-        def a(k):
-            wait("v", arr[k])
-            o = (m * 8 + k) * MS + 32
-            ta[k] = V_(ve.tensor_scalar(T.colu[:, 2 * k:2 * k + 2], T.land[:, o:o + 2], 8.0, float((rank - k) % N),
-                                        A.mult, A.add))
+        def a(k0, k1):
+            wait("v", *arr[k0:k1])
+            ta[k1 - 1] = V_(ve.tensor_scalar(
+                T.colu[:, 2 * k0:2 * k1], T.land[:, (m * 8 + k0) * MS:(m * 8 + k1) * MS:MS // 2],
+                4.0, float(4 * VV + (rank ^ k0) // 2), A.mult, A.add))
 
         def b(k0, k1):
             wait("v", ta[k1 - 1], st["post"])
@@ -257,12 +261,11 @@ def rank_program(g, core, T, topo):
 
         b(0, 1)
         wait("v", last[0])
-        last[0] = V_(ve.tensor_copy(slots[:, 0:SL].indirect(T.offu[:, 0:2]), T.msg[:, m * MS:m * MS + 32]))
+        last[0] = V_(ve.tensor_copy(slots[:, 0:SL].indirect(T.offu[:, 0:2]), T.msg[:, m * MS + 1:m * MS + 33]))
         d(0, C0); d(C0, 32)
-        a(1); b(1, 2); d(32, 32 + C1); a(2); a(3); d(32 + C1, 64)
-        b(2, 4); a(4); a(5); d(64, 128)
-        b(4, 6); a(6); a(7); d(128, 192)
-        b(6, 8); d(192, 256)
+        a(1, 2); b(1, 2); a(2, 4); d(32, 64)
+        b(2, 4); a(4, 6); a(6, 8); d(64, 128)
+        b(4, 8); d(128, 256)
         return last[0]
 
     wait("v", t_x0)
@@ -278,9 +281,7 @@ def rank_program(g, core, T, topo):
 
     def dchunk(c):
         ps = T.psa if c % 2 == 0 else T.psb
-        wait("t", st["dq"], st["sel"])
-        if c == 1:
-            wait("t", st["post"])
+        wait("t", st["sel"], st["se"])
         if c >= 2:
             wait("t", s_d[c - 2])
         for lo, hi in ((0, 512), (512, 1024), (1024, CH)):
@@ -295,7 +296,6 @@ def rank_program(g, core, T, topo):
 
     def setup():
         wait("g", G_(g.iota(T.zb[:], [[0, 128 * (16 - ND)]], 0, 0, allow_small_or_imprecise_dtypes=True)))
-        st["gz"] = g_z0
         st["sel"] = G_(g.affine_select(T.sel[:], T.zb[:], [[-1, 16 - ND], [-16, 8], [0, 16]], A.not_equal, 1.0, -ND, 1))
         p_f = []
         fan1(1)
@@ -310,16 +310,17 @@ def rank_program(g, core, T, topo):
 
     def setup2():
         lo, hi = NP - ZV1, NP
+        V_(ve.tensor_tensor(T.xd[:], T.xm[:], T.drvi[:, V:2 * V], A.max))
         v_z = V_(ve.memset(slots[:, lo:hi], 0.0))
         wait("v", t_ci)
         v_cb = V_(ve.tensor_copy(T.cb[:], T.ci[:]))
         for q in range(N):
             wait("v", st["pf"][q // 4], g_du)
-            st["post"] = V_(ve.tensor_tensor(T.post[:, q:1024:8], T.fa[:, q * 128:(q + 1) * 128],
+            o = 4 * VV * (1 - q % 2)
+            st["post"] = V_(ve.tensor_tensor(T.post[:, o + q // 2:o + 4 * V:4], T.fa[:, q * 128:(q + 1) * 128],
                                              T.psb[:, q * 128:(q + 1) * 128], A.add))
         wait("t", v_cb, g_dm, s_d0)
-        ZS1 = lo - zc[0]
-        st["sz"] = zs(ZS1) if ZS1 else s_z
+        s_z = zs(lo - zc[0])
         for bk in range(3):
             for vl in range(3 * bk, min(8, 3 * bk + 3)):
                 o = bk * 512 + (vl % 3) * W
@@ -336,67 +337,89 @@ def rank_program(g, core, T, topo):
             for t in range(16):
                 st["db%d" % w] = inc("lb%d" % w, sy.dma_start(D[t:128:16, lo:hi], T.ddr[:, lo:hi]), 16)
         st["dr2"] = inc("ld2", sy.dma_start(T.drvi[:, 2 * V:640], T.drv[:, 2 * V:640]), 16)
-        wait("v", v_z, st["sz"], st["gz"], t_zd, t_dr1)
-        V_(ve.tensor_scalar(xo_ap, T.xc[:, 0:V], -float(DEC), None, A.add))
-        V_(ve.tensor_copy(dr_ap, T.drvi[:, V:2 * V]))
+        wait("v", v_z, s_z, g_z, t_zd)
+        V_(ve.tensor_copy(xo_ap, T.xd[:]))
 
-    toks = select(0, p_s, 0, lambda: zv(640), lambda: fan1(0), setup)
+    zv(640)
+    v_ch = changed(0, V, T.pss, p_s, 0)
+    V_(ve.tensor_scalar(T.xm[:], T.xc[:, 0:V], -float(DEC), None, A.add))
+    v_cum = counts(0, VV, v_ch)
+    fan1(0)
+    toks = select(0, v_cum, setup)
     setup2()
 
     for t in range(1, RO):
-        if t == 1:
-            for c in range(DE):
-                dchunk(c)
         v_last = push(t - 1, *toks)
         if t == 1:
-            for c in range(DE, 16 - ND):
+            for c in range(16 - ND):
                 dchunk(c)
-            pieces = [(ND * CH, (ND + DE) * CH, s_d[DE - 1])] if DE else []
-            late = [((ND + c) * CH, (ND + c + 2) * CH, s_d[c + 1]) for c in range(DE, 16 - ND, 2)]
-            pieces += [(0, ND // 2 * CH, st["db0"]), late[0], (ND // 2 * CH, ND * CH, st["db1"])] + late[1:]
+            late = [((ND + c) * CH, (ND + c + 2) * CH, s_d[c + 1]) for c in range(0, 16 - ND, 2)]
+            pieces = [(0, ND // 2 * CH, st["db0"]), late[0], (ND // 2 * CH, ND * CH, st["db1"])] + late[1:]
         else:
-            pieces = [(0, NP, v_last)]
+            pieces = [(0, VA * W, v_last), (VA * W, NP, v_last)]
+        parts = ((0, VA, T.pss), (VA, V, T.pst))
         wait("t", v_last, s_bh)
-        p_l = P_(te.matmul(T.pss[:, 0:V], T.bh[:], la_ap, True, False))
+        for lo, hi, ps in parts:
+            P_(te.matmul(ps[:, lo:hi], T.bh[:], slots[:, lo * W + 129:hi * W:W], True, False))
         wait("v", v_last)
+        scans = []
         for lo, hi, tok in pieces:
             wait("v", tok)
-            v_scan = V_(ve.tensor_tensor_scan(outb[:, lo:hi], D[:, lo:hi], slots[:, lo:hi], 0.0, A.add, A.max))
-        wait("t", v_scan)
-        P_(te.matmul(T.pss[:, 0:V], T.bh[:], xn_ap, False, False))
-        p_s = P_(te.matmul(T.pss[:, 0:V], T.bm[:], mx_ap, False, True))
+            scans.append(V_(ve.tensor_tensor_scan(outb[:, lo:hi], D[:, lo:hi], slots[:, lo:hi], 0.0, A.add, A.max)))
+        v_scan, p_s = scans[-1], []
+        for (lo, hi, ps), tok in zip(parts, scans[-2:]):
+            wait("t", tok)
+            P_(te.matmul(ps[:, lo:hi], T.bh[:], outb[:, lo * W + 128:hi * W:W], False, False))
+            p_s.append(P_(te.matmul(ps[:, lo:hi], T.bm[:], outb[:, lo * W + 129:hi * W:W], False, True)))
+        v_a = changed(0, VA, T.pss, p_s[0], 1)
         if t < RO - 1:
-            def g1():
-                wait("v", v_scan, p_l)
-                V_(ve.tensor_copy(T.xc[:, 0:V], xn_ap))
-                V_(ve.tensor_scalar(xo_ap, xn_ap, -float(DEC), None, A.add))
-
-            def g2():
-                wait("v", st["dr2"])
-                V_(ve.tensor_copy(dr_ap, T.drvi[:, (t + 1) * V:(t + 2) * V]))
-
-            toks = select(t, p_s, 1, g1, g2, lambda: None)
+            wait("v", v_scan)
+            V_(ve.tensor_copy(T.xc[:, 0:V], xn_ap))
+            v_ca = counts(0, VA, v_a)
+            v_b = changed(VA, V, T.pst, p_s[1], 1)
+            v_xm = V_(ve.tensor_scalar(T.xm[:], xn_ap, -float(DEC), None, A.add))
+            v_cum = counts(VA, VV, v_ca, v_b)
+            wait("v", v_xm, st["dr2"])
+            V_(ve.tensor_tensor(xo_ap, T.xm[:], T.drvi[:, (t + 1) * V:(t + 2) * V], A.max))
+            toks = select(t, v_cum, lambda: None)
         else:
             wait("s", v_scan)
             s_x = S_(sc.activation(T.yxf[:], xn_ap, F.Copy))
             wait("s", s_x)
             inc("ox", sc.dma_start(T.yx[:], T.yxf[:]), 16)
             wait("v", v_scan)
-            V_(ve.tensor_tensor(T.dif[:], xn_ap, la_ap, A.subtract))
-            wait("v", p_s)
-            v_ch = V_(ve.tensor_scalar(T.ch[:, 0:V], T.pss[:, 0:V], T.thf[:, 1:2], None, A.is_ge))
-            wait("v", v_ch)
-            v_cum = V_(ve.tensor_tensor_scan(T.cum[:, 0:V], T.ch[:, 0:V], T.ch[:, 0:V], 0.0, A.add, A.max))
-            V_(ve.tensor_tensor(T.psa[:, 0:V], T.ch[:, 0:V], T.dif[:], A.mult))
-            wait("v", v_cum)
-            v_u = V_(ve.tensor_scalar(T.uu[:], T.cum[:, 0:V], float(CAP), None, A.is_le))
-            wait("v", v_u)
-            v_t = V_(ve.tensor_tensor(T.psb[:, 0:V], T.uu[:], T.psa[:, 0:V], A.mult))
-            wait("v", v_t)
-            v_l = V_(ve.tensor_tensor(T.ylf[:], T.psb[:, 0:V], la_ap, A.add))
+            v_df = V_(ve.tensor_tensor(T.dif[:], xn_ap, la_ap, A.subtract))
+
+            def kept(lo, hi, tok):
+                wait("v", tok)
+                return V_(ve.tensor_tensor(T.psa[:, lo:hi], T.ch[:, lo:hi], T.dif[:, lo:hi], A.mult))
+
+            def first(lo, hi, tok):
+                wait("v", tok)
+                return V_(ve.tensor_scalar(T.uu[:, lo:hi], T.cum[:, lo:hi], float(CAP), None, A.is_le))
+
+            def both(lo, hi, tok):
+                wait("v", tok)
+                return V_(ve.tensor_tensor(T.psb[:, lo:hi], T.uu[:, lo:hi], T.psa[:, lo:hi], A.mult))
+
+            def new_last(lo, hi, tok):
+                wait("v", tok)
+                return V_(ve.tensor_tensor(T.ylf[:, lo:hi], T.psb[:, lo:hi], slots[:, lo * W + 129:hi * W:W], A.add))
+
+            v_ca = counts(0, VA, v_a)
+            v_b = changed(VA, V, T.pst, p_s[1], 1)
+            kept(0, VA, v_df)
+            v_cum = counts(VA, V, v_b, v_ca)
+            v_ua = first(0, VA, v_ca)
+            kept(VA, V, v_b)
+            v_ub = first(VA, V, v_cum)
+            v_ta = both(0, VA, v_ua)
+            v_tb = both(VA, V, v_ub)
+            new_last(0, VA, v_ta)
+            v_l = new_last(VA, V, v_tb)
             wait("y", v_l)
             inc("ol", sy.dma_start(T.yl[:], T.ylf[:]), 16)
 
     for name in SEMAPHORES:
-        if name in count and name[0] != "a":
+        if name in count:
             wait("g", (name, count[name]))

from concourse.bass import DstId, RemoteDMATransfer
from concourse.mybir import AluOpType, ActivationFunctionType

N, V, CAP, RO, DEC = 8, 128, 32, 5, 8
W = 130
NP = V * W
SPARE = 20992
SL = 25216
VV = V + CAP
MS = 80
MW = 41
VA = V - 16
CH = 8 * W
ND = 8
C0 = 8
ZD, ZG0 = 8192, 384
ZV0, ZV1 = 1792, 896
ZS0 = 128
POFF = 129 * (128 * W - 1)

SCRATCH = {
    "slots": ("sbuf", [128, SL], "bfloat16"),
    "dd": ("sbuf", [128, NP], "bfloat16"),
    "outb": ("sbuf", [128, NP], "bfloat16"),
    "fani": ("sbuf", [128, 1024], "int32"),
    "fa": ("sbuf", [128, 1024], "float32"),
    "fh": ("sbuf", [128, 1024], "bfloat16"),
    "zb": ("sbuf", [128, 128 * (16 - ND)], "bfloat16"),
    "nid": ("sbuf", [128, 128], "bfloat16"),
    "post": ("sbuf", [128, 8 * VV], "float32"),
    "ci": ("sbuf", [128, 1024], "int32"),
    "cb": ("sbuf", [128, 1024], "bfloat16"),
    "dq": ("sbuf", [128, CH], "bfloat16"),
    "ddr": ("dram", [8, NP], "bfloat16"),
    "x0i": ("sbuf", [128, 128], "int32"),
    "drvi": ("sbuf", [128, 640], "int32"),
    "thi": ("sbuf", [128, 4], "int32"),
    "thf": ("sbuf", [128, 4], "float32"),
    "xm": ("sbuf", [128, 128], "bfloat16"),
    "xd": ("sbuf", [128, 128], "bfloat16"),
    "xc": ("sbuf", [128, VV], "bfloat16"),
    "ch": ("sbuf", [128, VV], "bfloat16"),
    "cum": ("sbuf", [128, VV], "bfloat16"),
    "junk": ("sbuf", [128, 2 * VV], "bfloat16"),
    "acc": ("sbuf", [128, 8], "float32"),
    "idxu": ("sbuf", [128, 8], "uint16"),
    "colu": ("sbuf", [128, 16], "uint16"),
    "offu": ("sbuf", [128, 258], "uint16"),
    "vexp": ("sbuf", [128, 4096], "bfloat16"),
    "msg": ("sbuf", [128, 4 * MS], "bfloat16"),
    "land": ("sbuf", [128, 4 * 8 * MS], "bfloat16"),
    "bm": ("sbuf", [128, 128], "bfloat16"),
    "bh": ("sbuf", [128, 128], "bfloat16"),
    "mg": ("sbuf", [128, 128], "bfloat16"),
    "dm1": ("sbuf", [128, 136], "bfloat16"),
    "dm": ("sbuf", [128, 136], "bfloat16"),
    "sel": ("sbuf", [128, 128 * (16 - ND)], "bfloat16"),
    "pc": ("sbuf", [128, 4], "int32"),
    "colf": ("sbuf", [128, 4], "float32"),
    "exi": ("sbuf", [128, 32], "int32"),
    "exu": ("sbuf", [128, 32], "uint16"),
    "yxf": ("sbuf", [128, 128], "float32"),
    "ylf": ("sbuf", [128, 128], "float32"),
    "dif": ("sbuf", [128, 128], "bfloat16"),
    "uu": ("sbuf", [128, 128], "bfloat16"),
    "psa": ("psum", [128, 1536], "float32"),
    "psb": ("psum", [128, 1536], "float32"),
    "pss": ("psum", [128, 512], "float32"),
    "pst": ("psum", [128, 512], "float32"),
}
SEMAPHORES = (["sv", "ss", "st", "sg", "lx", "ld", "lt", "lc", "lf", "lf1", "ld2", "lq", "lb0", "lb1", "lz", "ox", "ol",
               "sent0", "sent1"] + ["a%d_%d" % (m, k) for m in range(4) for k in range(N)])


def rank_program(g, core, T, topo):
    rank = T.rank_of(core)
    if rank is None:
        return
    A, F = AluOpType, ActivationFunctionType
    ve, sc, te, sy = g.vector, g.scalar, g.tensor, g.sync
    Q = {"v": ve, "s": sc, "t": te, "y": sy, "g": g}
    count = {}
    seen = {q: {} for q in Q}

    def wait(q, *toks):
        most = {}
        for name, val in toks:
            most[name] = max(most.get(name, 0), val)
        for name, val in most.items():
            if seen[q].get(name, 0) < val:
                Q[q].wait_ge(T.sem[name], val)
                seen[q][name] = val

    def inc(name, ins, n=1):
        ins.then_inc(T.sem[name], n)
        count[name] = count.get(name, 0) + n
        return (name, count[name])

    def V_(ins):
        return inc("sv", ins)

    def S_(ins):
        return inc("ss", ins)

    def P_(ins):
        return inc("st", ins)

    def G_(ins):
        return inc("sg", ins)

    slots, D, outb = T.slots, T.dd, T.outb
    xo_ap = slots[:, 128:NP:W]
    la_ap = slots[:, 129:NP:W]
    xn_ap = outb[:, 128:NP:W]

    t_x0 = inc("lx", sy.dma_start(T.x0i[:], T.x0[:]), 16)
    t_dr = inc("ld", sc.dma_start(T.drvi[:, 0:2 * V], T.drv[:, 0:2 * V]), 16)
    t_th = inc("lt", sc.dma_start(T.thi[:, 0:1], T.th[:]), 16)
    t_fan = [inc(n, sy.dma_start(T.fani[:, h * 512:(h + 1) * 512], T.fan[:, h * 512:(h + 1) * 512]), 16)
             for h, n in enumerate(("lf", "lf1"))]
    for n in range(8):
        t_ci = inc("lc", sy.dma_start(T.ci[:, n * 128:(n + 1) * 128], T.cost[n]), 16)

    zc = [2048]

    def take(n):
        lo = zc[0]
        zc[0] = min(NP, lo + n)
        return lo, zc[0]

    def zv(n):
        lo, hi = take(n)
        return V_(ve.memset(slots[:, lo:hi], 0.0))

    def zs(n):
        for k in range(0, n, 1024):
            lo, hi = take(min(1024, n - k))
            t = S_(sc.activation(slots[:, lo:hi], slots[:, 0:hi - lo], F.Copy))
        return t

    z1 = V_(ve.memset(slots[:, 0:1024], 0.0))
    wait("v", ("sg", 1))
    v1 = V_(ve.tensor_scalar(T.pc[:, 2:3], T.pc[:, 0:1], 15, None, A.bitwise_and))
    t_zd = z2 = V_(ve.memset(slots[:, 1024:2048], 0.0))
    for n in range(0, ZD, 2048):
        wait("y", z2)
        lo, hi = take(min(2048, ZD - n))
        t_zd = inc("lz", sy.dma_start(slots[:, lo:hi], slots[:, 0:hi - lo]), 16)

    G_(g.iota(T.pc[:, 0:1], [[0, 1]], 0, 1))
    g_ex = G_(g.iota(T.exi[:], [[1, 32]], 1, 0))
    for h in range(2):
        g_du = G_(g.iota(T.post[:, 640 * h + 512:640 * h + 640], [[16, 128]], SPARE + 2048 * h - POFF, 1,
                         allow_small_or_imprecise_dtypes=True))
    wait("g", z1)
    g_b1 = G_(g.affine_select(T.mg[:], slots[:, 0:128], [[16, 8], [0, 16]], A.is_gt, 1.0, 0, -1))
    g_d1 = G_(g.affine_select(T.dm1[:, 0:W], slots[:, 0:W], [[1, W]], A.not_equal, 1.0, 0, -1))
    wait("g", g_b1)
    g_bm = G_(g.affine_select(T.bm[:], T.mg[:], [[16, 8], [0, 16]], A.is_ge, 0.0, 15, -1))
    wait("g", g_d1)
    g_dm = G_(g.affine_select(T.dm[:, 0:W], T.dm1[:, 0:W], [[1, W]], A.not_equal, -1.0, -1, -1))
    lo, hi = take(ZG0)
    g_z = G_(g.iota(slots[:, lo:hi], [[0, hi - lo]], 0, 0, allow_small_or_imprecise_dtypes=True))

    wait("v", v1, g_ex)
    v2 = V_(ve.tensor_scalar(T.colf[:, 1:2], T.pc[:, 2:3], 0.5, None, A.add))
    v_ex = V_(ve.tensor_copy(T.exu[:, 0:32], T.exi[:]))
    zv(ZV0)
    wait("s", z1)
    S_(sc.activation(T.xc[:, V:VV], slots[:, 0:CAP], F.Copy))
    s_ms = S_(sc.activation(T.msg[:], slots[:, 0:4 * MS], F.Copy))
    s_ch = S_(sc.activation(T.ch[:, V:VV], slots[:, 0:CAP], F.Copy, bias=1.0))
    for bk in range(3):
        s_d0 = S_(sc.activation(T.psa[:, bk * 512:bk * 512 + 3 * W:W], slots[:, 0:3], F.Copy, bias=-512.0))
    zs(1024)
    wait("s", v2)
    s_c2 = S_(sc.activation(T.colf[:, 2:3], T.colf[:, 1:2], F.Copy, bias=16.0))
    zs(768)
    wait("s", g_bm)
    s_bh = S_(sc.activation(T.bh[:], T.bm[:], F.Copy, scale=-0.5))
    wait("s", g_d1)
    s_ni = S_(sc.activation(T.nid[:], T.dm1[:, 0:128], F.Copy, scale=-float(128 * W)))
    zs(ZS0)

    peers = [T.cores[rank ^ k] for k in range(N)]
    ids = [DstId(rid=topo.addr(d, core)[0], pnc=topo.addr(d, core)[1]) for d in peers[1:]]
    odd = rank % 2
    st = {}

    def changed(lo, hi, ps, tok, thcol):
        wait("v", tok)
        return V_(ve.tensor_scalar(T.ch[:, lo:hi], ps[:, lo:hi], T.thf[:, thcol:thcol + 1], None, A.is_ge))

    def counts(lo, hi, *toks):
        wait("v", s_ch, *toks)
        return V_(ve.tensor_tensor_scan(T.cum[:, lo:hi], T.ch[:, lo:hi], T.ch[:, lo:hi],
                                        T.cum[:, lo - 1:lo] if lo else 0.0, A.add, A.max))

    def select(m, v_cum, after_send):
        wait("s", v_cum, s_c2)
        for h in range(2):
            s_acc = S_(sc.activation(T.junk[:, h * VV:(h + 1) * VV], T.cum[:], F.Sign, bias=T.colf[:, 1 + h:2 + h],
                                     scale=-1.0, accum_out=T.acc[:, 2 * m + h:2 * m + h + 1]))
        acc = T.acc[:, 2 * m:2 * m + 2]
        wait("s", s_acc)
        s_idx = S_(sc.activation(T.msg[:, m * MS:m * MS + MW:MS // 2], acc, F.Copy, bias=float(VV // 2 - odd * VV), scale=0.5))
        wait("v", s_acc)
        v_idx = V_(ve.tensor_scalar(T.idxu[:, 2 * m:2 * m + 2], acc, 0.5, float(VV // 2), A.mult, A.add))
        v_col = V_(ve.tensor_scalar(T.colu[:, 0:2], acc, 2.0, float(2 * VV + 4 * VV * (1 - odd) + rank // 2), A.mult, A.add))
        V_(ve.tensor_scalar(T.offu[:, 0:2], acc, W / 2.0, float(VV // 2 * W + W - 1), A.mult, A.add))
        wait("v", v_idx)
        v_val = V_(ve.tensor_copy(T.msg[:, m * MS + 1:m * MS + 33], T.xc[:, 0:VV].indirect(T.idxu[:, 2 * m:2 * m + 2])))
        wait("g", s_idx, v_val)
        sent = "sent0" if m == 0 else "sent1"
        g.remote_dma_fused([RemoteDMATransfer(
            dst_ids=ids, dma_engine_mask=topo.mask(core, peers[1]), remote_sem=T.sem["a%d_%d" % (m, rank)],
            srcs=[T.msg[:, m * MS:m * MS + MW]],
            dsts=[T.land[:, (m * 8 + k) * MS:(m * 8 + k) * MS + MW] for k in range(1, N)])], local_sem=T.sem[sent])
        count[sent] = count.get(sent, 0) + len(topo.engines(core, peers[1]))
        after_send()
        wait("s", v_val, v_ex, s_idx)
        own = T.msg[:, m * MS:m * MS + 33]
        s_e0 = (S_(sc.activation(T.vexp[:, 0:16 * C0], own.indirect(T.exu[:, 0:C0]), F.Copy)),
                S_(sc.activation(T.vexp[:, 16 * C0:512], own.indirect(T.exu[:, C0:32]), F.Copy)))
        return v_col, s_e0

    def push(m, v_col, s_e0):
        s_e = {C0: s_e0[0], 32: s_e0[1]}
        arr = [None] + [("a%d_%d" % (m, rank ^ k), len(topo.engines(peers[k], core))) for k in range(1, N)]
        for k in range(1, 3):
            wait("s", arr[k])
            win = T.land[:, (m * 8 + k) * MS:(m * 8 + k) * MS + 33]
            s_e[32 * k + 32] = S_(sc.activation(T.vexp[:, 512 * k:512 * k + 512], win.indirect(T.exu[:, 0:32]), F.Copy))
        wait("t", st["post"], st["dq"])
        for k0, k1, ps, c in ((3, 4, T.psa, 0), (4, 6, T.psa, 512), (6, 8, T.psb, 0)):
            for k in range(k0, k1):
                wait("t", arr[k])
                o, b0 = (m * 8 + k) * MS, c + 512 * (k - k0)
                for i in range(16):
                    p_e = P_(te.matmul(ps[:, b0 + i:b0 + 512:16], T.dm1[:, 0:128], T.land[:, o + 1:o + 33], True, True))
            wait("s", p_e)
            st["se"] = s_e[32 * k1] = S_(sc.activation(T.vexp[:, 512 * k0:512 * k1], ps[:, c:c + 512 * (k1 - k0)], F.Copy))
        ta, tb, last = {0: v_col}, {}, [("sv", count["sv"])]

        def a(k0, k1):
            wait("v", *arr[k0:k1])
            ta[k1 - 1] = V_(ve.tensor_scalar(
                T.colu[:, 2 * k0:2 * k1], T.land[:, (m * 8 + k0) * MS:(m * 8 + k1) * MS:MS // 2],
                4.0, float(4 * VV + (rank ^ k0) // 2), A.mult, A.add))

        def b(k0, k1):
            wait("v", ta[k1 - 1], st["post"])
            t = V_(ve.tensor_scalar(T.offu[:, 2 + 32 * k0:2 + 32 * k1], T.post[:].indirect(T.colu[:, 2 * k0:2 * k1]),
                                    float(POFF), None, A.add))
            for k in range(k0, k1):
                tb[k] = t

        def d(c0, c1):
            wait("v", tb[(c1 - 1) // 32], s_e[c1], last[0])
            last[0] = V_(ve.tensor_copy(slots[:, 0:SL].indirect(T.offu[:, 2 + c0:2 + c1]), T.vexp[:, 16 * c0:16 * c1]))

        b(0, 1)
        wait("v", last[0])
        last[0] = V_(ve.tensor_copy(slots[:, 0:SL].indirect(T.offu[:, 0:2]), T.msg[:, m * MS + 1:m * MS + 33]))
        d(0, C0); d(C0, 32)
        a(1, 2); b(1, 2); a(2, 4); d(32, 64)
        b(2, 4); a(4, 6); a(6, 8); d(64, 128)
        b(4, 8); d(128, 256)
        return last[0]

    wait("v", t_x0)
    v_xm = V_(ve.tensor_scalar(T.xm[:], T.x0i[:], -float(DEC), None, A.add))
    wait("v", t_th)
    V_(ve.tensor_copy(T.thf[:, 0:1], T.thi[:, 0:1]))
    V_(ve.tensor_scalar(T.thf[:, 1:2], T.thi[:, 0:1], 0.5, None, A.mult))
    wait("v", t_dr, v_xm)
    v_x = V_(ve.tensor_tensor(T.xc[:, 0:V], T.xm[:], T.drvi[:, 0:V], A.max))
    wait("t", v_x, g_bm)
    p_s = P_(te.matmul(T.pss[:, 0:V], T.bm[:], T.xc[:, 0:V], True, True))
    s_d = []

    def dchunk(c):
        ps = T.psa if c % 2 == 0 else T.psb
        wait("t", st["sel"], st["se"])
        if c >= 2:
            wait("t", s_d[c - 2])
        for lo, hi in ((0, 512), (512, 1024), (1024, CH)):
            p_d = P_(te.matmul(ps[:, lo:hi], T.sel[:, c * 128:(c + 1) * 128], T.dq[:, lo:hi], True, True))
        wait("s", p_d)
        s_d.append(S_(sc.activation(D[:, (ND + c) * CH:(ND + c + 1) * CH], ps[:, 0:CH], F.Copy)))

    def fan1(h):
        wait("v", t_fan[h])
        c = slice(h * 512, (h + 1) * 512)
        st["fa%d" % h] = V_(ve.tensor_scalar(T.fa[:, c], T.fani[:, c], float(W), None, A.mult))

    def setup():
        wait("g", G_(g.iota(T.zb[:], [[0, 128 * (16 - ND)]], 0, 0, allow_small_or_imprecise_dtypes=True)))
        st["sel"] = G_(g.affine_select(T.sel[:], T.zb[:], [[-1, 16 - ND], [-16, 8], [0, 16]], A.not_equal, 1.0, -ND, 1))
        p_f = []
        fan1(1)
        for h in range(2):
            c = slice(h * 512, (h + 1) * 512)
            wait("s", st["fa%d" % h])
            s_h = S_(sc.activation(T.fh[:, c], T.fa[:, c], F.Copy, bias=128.504, scale=1.0 / (128 * W)))
            wait("t", s_h, s_ni)
            P_(te.matmul(T.psb[:, c], T.nid[:], T.fh[:, c], True, False))
            p_f.append(P_(te.matmul(T.psb[:, c], T.dm1[:, 0:128], T.fh[:, c], False, True)))
        st["pf"] = p_f

    def setup2():
        lo, hi = NP - ZV1, NP
        V_(ve.tensor_tensor(T.xd[:], T.xm[:], T.drvi[:, V:2 * V], A.max))
        v_z = V_(ve.memset(slots[:, lo:hi], 0.0))
        wait("v", t_ci)
        v_cb = V_(ve.tensor_copy(T.cb[:], T.ci[:]))
        for q in range(N):
            wait("v", st["pf"][q // 4], g_du)
            o = 4 * VV * (1 - q % 2)
            st["post"] = V_(ve.tensor_tensor(T.post[:, o + q // 2:o + 4 * V:4], T.fa[:, q * 128:(q + 1) * 128],
                                             T.psb[:, q * 128:(q + 1) * 128], A.add))
        wait("t", v_cb, g_dm, s_d0)
        s_z = zs(lo - zc[0])
        for bk in range(3):
            for vl in range(3 * bk, min(8, 3 * bk + 3)):
                o = bk * 512 + (vl % 3) * W
                p_q = P_(te.matmul(T.psa[:, o + 1:o + W], T.cb[:, vl:1024:8], T.dm[:, 1:W], True, True))
            wait("s", p_q)
            n = min(3 * W, CH - bk * 3 * W)
            s_q = S_(sc.activation(T.dq[:, bk * 3 * W:bk * 3 * W + n], T.psa[:, bk * 512:bk * 512 + n], F.Copy))
        st["dq"] = s_q
        wait("y", s_q)
        t_q = inc("lq", sy.dma_start(T.ddr[:], T.dq[:]), 16)
        wait("y", t_q)
        for w in range(2):
            lo, hi = w * ND // 2 * CH, (w + 1) * ND // 2 * CH
            for t in range(16):
                st["db%d" % w] = inc("lb%d" % w, sy.dma_start(D[t:128:16, lo:hi], T.ddr[:, lo:hi]), 16)
        st["dr2"] = inc("ld2", sy.dma_start(T.drvi[:, 2 * V:640], T.drv[:, 2 * V:640]), 16)
        wait("v", v_z, s_z, g_z, t_zd)
        V_(ve.tensor_copy(xo_ap, T.xd[:]))

    zv(640)
    v_ch = changed(0, V, T.pss, p_s, 0)
    V_(ve.tensor_scalar(T.xm[:], T.xc[:, 0:V], -float(DEC), None, A.add))
    v_cum = counts(0, VV, v_ch)
    fan1(0)
    toks = select(0, v_cum, setup)
    setup2()

    for t in range(1, RO):
        v_last = push(t - 1, *toks)
        if t == 1:
            for c in range(16 - ND):
                dchunk(c)
            late = [((ND + c) * CH, (ND + c + 2) * CH, s_d[c + 1]) for c in range(0, 16 - ND, 2)]
            pieces = [(0, ND // 2 * CH, st["db0"]), late[0], (ND // 2 * CH, ND * CH, st["db1"])] + late[1:]
        else:
            pieces = [(0, VA * W, v_last), (VA * W, NP, v_last)]
        parts = ((0, VA, T.pss), (VA, V, T.pst))
        wait("t", v_last, s_bh)
        for lo, hi, ps in parts:
            P_(te.matmul(ps[:, lo:hi], T.bh[:], slots[:, lo * W + 129:hi * W:W], True, False))
        wait("v", v_last)
        scans = []
        for lo, hi, tok in pieces:
            wait("v", tok)
            scans.append(V_(ve.tensor_tensor_scan(outb[:, lo:hi], D[:, lo:hi], slots[:, lo:hi], 0.0, A.add, A.max)))
        v_scan, p_s = scans[-1], []
        for (lo, hi, ps), tok in zip(parts, scans[-2:]):
            wait("t", tok)
            P_(te.matmul(ps[:, lo:hi], T.bh[:], outb[:, lo * W + 128:hi * W:W], False, False))
            p_s.append(P_(te.matmul(ps[:, lo:hi], T.bm[:], outb[:, lo * W + 129:hi * W:W], False, True)))
        v_a = changed(0, VA, T.pss, p_s[0], 1)
        if t < RO - 1:
            wait("v", v_scan)
            V_(ve.tensor_copy(T.xc[:, 0:V], xn_ap))
            v_ca = counts(0, VA, v_a)
            v_b = changed(VA, V, T.pst, p_s[1], 1)
            v_xm = V_(ve.tensor_scalar(T.xm[:], xn_ap, -float(DEC), None, A.add))
            v_cum = counts(VA, VV, v_ca, v_b)
            wait("v", v_xm, st["dr2"])
            V_(ve.tensor_tensor(xo_ap, T.xm[:], T.drvi[:, (t + 1) * V:(t + 2) * V], A.max))
            toks = select(t, v_cum, lambda: None)
        else:
            wait("s", v_scan)
            s_x = S_(sc.activation(T.yxf[:], xn_ap, F.Copy))
            wait("s", s_x)
            inc("ox", sc.dma_start(T.yx[:], T.yxf[:]), 16)
            wait("v", v_scan)
            v_df = V_(ve.tensor_tensor(T.dif[:], xn_ap, la_ap, A.subtract))

            def kept(lo, hi, tok):
                wait("v", tok)
                return V_(ve.tensor_tensor(T.psa[:, lo:hi], T.ch[:, lo:hi], T.dif[:, lo:hi], A.mult))

            def first(lo, hi, tok):
                wait("v", tok)
                return V_(ve.tensor_scalar(T.uu[:, lo:hi], T.cum[:, lo:hi], float(CAP), None, A.is_le))

            def both(lo, hi, tok):
                wait("v", tok)
                return V_(ve.tensor_tensor(T.psb[:, lo:hi], T.uu[:, lo:hi], T.psa[:, lo:hi], A.mult))

            def new_last(lo, hi, tok):
                wait("v", tok)
                return V_(ve.tensor_tensor(T.ylf[:, lo:hi], T.psb[:, lo:hi], slots[:, lo * W + 129:hi * W:W], A.add))

            v_ca = counts(0, VA, v_a)
            v_b = changed(VA, V, T.pst, p_s[1], 1)
            kept(0, VA, v_df)
            v_cum = counts(VA, V, v_b, v_ca)
            v_ua = first(0, VA, v_ca)
            kept(VA, V, v_b)
            v_ub = first(VA, V, v_cum)
            v_ta = both(0, VA, v_ua)
            v_tb = both(VA, V, v_ub)
            new_last(0, VA, v_ta)
            v_l = new_last(VA, V, v_tb)
            wait("y", v_l)
            inc("ol", sy.dma_start(T.yl[:], T.ylf[:]), 16)

    for name in SEMAPHORES:
        if name in count:
            wait("g", (name, count[name]))
